import numpy as np, ml_dtypes
CORES = [16,17,18,19,32,33,34,35]
N = 8
BF = ml_dtypes.bfloat16
def gentries(a):
    return np.ascontiguousarray(a.reshape(8, 16, -1).transpose(0, 2, 1)).reshape(8, -1)
def gtable(e):
    e = np.asarray(e); return np.ascontiguousarray(e.reshape(8, -1, 16).transpose(0, 2, 1)).reshape(128, -1).astype(np.int32)
M, L, T, H, A, R = 2048, 192, 4, 2048, 10, 1024
W = M + L * T; NONE = 4095
def hashes(w, a):
    u = np.matmul(w.transpose(0, 2, 1), a) & 4095
    return (((u[:, 0] * u[:, 1]) >> 5) + u[:, 1]) & (H - 1)
def some(rng, n, tops):
    return (rng.random((N, 8, 16, n)) * rng.choice(np.array(tops), (N, 8, 1, n))).astype(np.int64)
def places(rng, sizes):
    v = np.zeros((N, 8, L), np.int64)
    for r in range(N):
        for g in range(8):
            pool = rng.permutation(M)[:int(sizes[r, g])]; v[r, g] = pool[rng.integers(0, len(pool), L)]
    return v
def flat(a):
    return np.ascontiguousarray(a.reshape(N, 128, -1)).astype(np.float32).astype(BF)
def pack(X, B, E, x, v, w):
    return {"nodes": flat(X), "book": flat(B), "kids": np.ascontiguousarray(E.reshape(N, 128, M)).astype(np.int32), "cand": flat(x),
            "spot": np.stack([gtable(a) for a in v]), "wts": flat(w)}
def setup_inputs(rng):
    X = some(rng, M, (48, 96, 160, 256)); B = some(rng, H, (96, 160, 256)); x = some(rng, L, (96, 192, 256))
    k = np.minimum(rng.integers(0, 17, (N, 8, 16, M)), rng.integers(0, 17, (N, 8, 16, M)))
    fill = rng.choice(np.array([0.3, 0.6, 0.9, 1.0]), (N, 8, 1, M))
    E = 4096 * k + np.where(rng.random((N, 8, 16, M)) < fill, rng.integers(0, M, (N, 8, 16, M)), NONE)
    v = places(rng, rng.choice(np.array([8, 32, 128, M]), (N, 8)))
    return pack(X, B, E, x, v, rng.integers(0, 16, (N, 8, 16, 2)))
def setup_inputs_spread(rng):
    X = (np.exp2(8 * rng.random((N, 8, 1, M))) * rng.random((N, 8, 16, M))).astype(np.int64)
    x = (np.exp2(8 * rng.random((N, 8, 1, L))) * rng.random((N, 8, 16, L))).astype(np.int64); B = rng.integers(0, 256, (N, 8, 16, H))
    E = 4096 * rng.integers(0, 17, (N, 8, 16, M)) + np.where(rng.random((N, 8, 16, M)) < rng.random((N, 8, 1, M)), rng.integers(0, M, (N, 8, 16, M)), NONE)
    v = np.minimum((M * rng.random((N, 8, L)) ** 3).astype(np.int64), M - 1); w = np.minimum((16 * rng.random((N, 8, 16, 2)) ** 2).astype(np.int64), 15)
    return pack(X, B, E, x, v, w)
def setup_inputs_ends(rng):
    X = 255 * rng.integers(0, 2, (N, 8, 16, M)); B = 255 * rng.integers(0, 2, (N, 8, 16, H)); x = 255 * rng.integers(0, 2, (N, 8, 16, L))
    a = rng.random((N, 8, 1, L)); x = np.where(a < 0.15, 0, np.where(a < 0.4, 255, x))
    X[..., 0] = 0; X[..., M - 1] = 255
    w = 15 * rng.integers(0, 2, (N, 8, 16, 2)); w[:, ::2, 13] = 15; w[:, ::2, 14] = 1; w[:, ::2, 15] = 15; w[:, 7] = 15
    E = 69631 * rng.integers(0, 2, (N, 8, 16, M)); o = rng.random(E.shape)
    E = np.where(o < 0.35, rng.choice(np.array([65536, M - 1, M - 1 + 65536]), E.shape), E)
    E = np.where(o < 0.1, rng.integers(1, M - 16, E.shape) + 65536 * rng.integers(0, 2, E.shape), E)
    E[..., M - 1] = 69631 * rng.integers(0, 2, (N, 8, 16)); E[:, :, 15, M - 1] = M - 1 + 65536; low = rng.integers(0, 8, (N, 8))
    E[:, :, :15, M - 2] = 0; E[:, :, 15, M - 2] = 69631
    for j in range(1, T): E[:, :, :, M - 2 - j] = 65536 + M - 1 - j
    E[:, :, :15, M - 2 - T] = 69631; E[:, :, 15, M - 2 - T] = 0
    v = np.where(rng.random((N, 8, L)) < 0.68, (M - 1) * rng.integers(0, 2, (N, 8, L)), rng.integers(1, M - 16, (N, 8, L)))
    v[:, :, L - 1] = M - 1 - T; x[..., L - 1] = 255
    v[:, :, L - 17] = M - 1; x[..., L - 17] = 255
    v[:, :, L - 33] = M - 2 - T; x[..., L - 33] = 255
    v[:, :, L - 2] = M - 1; x[:, ::2, :, L - 2] = 0; x[:, ::2, 14:, L - 2] = 255; x[:, ::2, 13, L - 2] = 1
    s = rng.integers(0, 2, (N, 8)); s[:, 7] = 1; s[:, 1] = 0
    for r in range(N):
        h = hashes(w[r], np.full((8, 16, 1), 255))[:, 0]
        for g in range(8):
            B[r, g, :, h[g]] = 255 * s[r, g]; E[r, g, low[r, g], M - 1] = 65536
    return pack(X, B, E, x, v, w)
def setup_inputs_corners(rng):
    X = some(rng, M, (2, 64, 256)); B = some(rng, H, (2, 128, 256))
    kind = rng.integers(0, 9, (N, 8, 1, M)); kind[..., 5:6 + T] = 4
    own = np.arange(M); one = rng.integers(0, 16, (N, 8, 1, M)); line = np.arange(16)[:, None]
    c = rng.integers(0, M, (N, 8, 16, M))
    c = np.where(kind == 3, own, np.where(kind == 4, (own + 1) % M, np.where(kind == 5, 0, np.where(kind == 6, M - 1, c))))
    hide = (kind == 0) | ((kind == 2) & (line != one)) | ((kind == 7) & (line == one)) | ((kind == 8) & (rng.random(c.shape) < 0.5))
    m = rng.integers(0, 4, (N, 8, 1, M)); m = np.where(kind == 4, 1, m)
    k = np.where(m == 0, 0, np.where(m == 1, 16, np.where(m == 2, 15, rng.integers(0, 17, c.shape))))
    E = 4096 * k + np.where(hide, NONE, c)
    v = rng.integers(0, M, (N, 8, L)); w = rng.integers(0, 16, (N, 8, 16, 2))
    for r in range(N):
        o = rng.permutation(8); q = rng.permutation(M)
        v[r, o[0]] = 0; v[r, o[1]] = M - 1; v[r, o[2]] = q[:L]; v[r, o[3]] = rng.permutation(np.repeat(q[:L // 2], 2))
        v[r, o[4]] = rng.choice(np.array([5, 0, M - 1, 6]), L); v[r, o[5], ::2] = 5; v[r, o[5], L - 1] = 5
        b = rng.permutation(8)
        w[r, b[0]] = 0; w[r, b[1]] = 15; w[r, b[2], 1:] = 0; w[r, b[2], 0] = 15; w[r, b[3], :15] = 0; w[r, b[3], 15] = 15; w[r, b[4], :, 0] = 0; w[r, b[5], :, 1] = 0
    d = rng.integers(0, 4, (N, 8, 1, L)); x = some(rng, L, (64, 256))
    x = np.where(d == 0, 0, np.where(d == 1, 255, np.where(d == 2, np.take_along_axis(X, v[:, :, None, :], 3), x)))
    return pack(X, B, E, x, v, w)
def full(rng, X, B, E, x, v, r, late):
    n = T - 1 if late else 0; half = rng.permutation(8)
    for g in range(8):
        u = rng.permutation(M)[:L * T].reshape(T, L); e = E[r, g]; v[r, g] = u[0]
        for j in range(n): e[:, u[j]] = 65536 + u[j + 1][None, :]
        if half[g] < 4:
            e[:, u[n]] = NONE + 4096 * rng.integers(0, 17, (16, L))
        else:
            X[r, g] = rng.integers(0, 8, (16, M)); x[r, g] = rng.integers(8, 24, (16, L)); B[r, g] = rng.integers(24, 256, (16, H))
            e[:, u[n]] = rng.integers(0, M, (16, L)) + 4096 * rng.integers(0, 16, (16, L))
def setup_inputs_crowd(rng):
    X = some(rng, M, (16, 64, 128)); B = some(rng, H, (160, 256)); x = np.minimum(some(rng, L, (128, 256)) + rng.integers(0, 64, (N, 8, 1, L)), 255)
    k = rng.integers(0, 17, (N, 8, 16, M)) * (rng.random((N, 8, 16, M)) < 0.3); fill = rng.choice(np.array([0.5, 1.0]), (N, 8, 1, M))
    E = 4096 * k + np.where(rng.random((N, 8, 16, M)) < fill, rng.integers(0, M, (N, 8, 16, M)), NONE)
    v = places(rng, rng.choice(np.array([1, 2, 3, 16]), (N, 8))); v[:, 0] = 0; v[:, 7] = M - 1
    o = rng.permutation(N); full(rng, X, B, E, x, v, int(o[0]), False); full(rng, X, B, E, x, v, int(o[1]), True)
    return pack(X, B, E, x, v, rng.integers(0, 16, (N, 8, 16, 2)))
def setup_inputs_ties(rng):
    X = 100 + rng.integers(0, 3, (N, 8, 16, M)); x = 100 + rng.integers(0, 3, (N, 8, 16, L)); B = rng.integers(0, 3, (N, 8, 16, H))
    c = rng.integers(0, M, (N, 8, 16, M)); c[:, ::2, 8:] = c[:, ::2, :8]
    E = 4096 * rng.integers(8, 15, c.shape) + np.where(rng.random(c.shape) < 0.8, c, NONE)
    v = places(rng, rng.choice(np.array([4, 16, 64, M]), (N, 8)))
    return pack(X, B, E, x, v, rng.integers(0, 16, (N, 8, 16, 2)))
def check_inputs(d):
    bad = []
    for k, lo, hi in (("nodes", 0, 255), ("book", 0, 255), ("kids", 0, 69631), ("cand", 0, 255), ("spot", 0, M - 1), ("wts", 0, 15)):
        a = np.asarray(d[k]).astype(np.float32)
        if not (np.min(a) >= lo and np.max(a) <= hi and np.all(a == np.floor(a))): bad.append("range of " + k)
    c = np.asarray(d["kids"]).astype(np.int64) & 4095
    if np.any((c >= M) & (c != NONE)): bad.append("children in kids")
    return bad
def reference(nodes, book, kids, cand, spot, wts):
    X = np.zeros((N, 8, 16, W), np.int64); X[..., :M] = nodes.astype(np.float32).astype(np.int64).reshape(N, 8, 16, M)
    E = np.full((N, 8, 16, W), NONE, np.int64); E[..., :M] = kids.astype(np.int64).reshape(N, 8, 16, M)
    B = book.astype(np.float32).astype(np.int64).reshape(N, 8, 16, H); w = wts.astype(np.float32).astype(np.int64).reshape(N, 8, 16, 2)
    xs = cand.astype(np.float32).astype(np.int64).reshape(N, 8, 16, L).copy(); vs = np.stack([gentries(a) for a in spot]).astype(np.int64)
    lane = np.arange(L); p = lane & 15; gr = np.arange(8)[:, None]
    for t in range(T):
        for r in range(N):
            x, v, q = xs[r], vs[r], (r + 1 + t % (N - 1)) % N
            ev = np.take_along_axis(E[r], v[:, None, :], 2)
            c = ev & 4095; thr = ev >> 12; filled = c != NONE
            xc = np.take_along_axis(X[r], np.where(filled, c, 0).reshape(8, 1, 16 * L), 2).reshape(8, 16, 16, L)
            dif = np.abs(x[:, :, None, :] - xc); fd = dif.reshape(8, 16, 16 * L)
            bc = np.take_along_axis(B[r], hashes(w[r], fd)[:, None, :], 2)
            s = np.add.reduce((bc >= fd).astype(np.int64), axis=1).reshape(8, 16, L)
            over = np.add.reduce((x[:, :, None, :] >= xc).astype(np.int64), axis=1)
            cap = filled & (over >= A) & (s > thr); stay = filled & ~cap
            go = stay[:, p, lane]
            best = np.argmax(np.where(stay, s, -1), axis=1)
            down = np.take_along_axis(c, best[:, None, :], 1)[:, 0]
            first = np.full((8, W), L); np.minimum.at(first, (gr, v), np.where(go, L, lane[None, :]))
            win = ~go & (first[gr, v] == lane[None, :]); wb = win[:, None, :]
            z = np.abs(np.take_along_axis(X[r], v[:, None, :], 2) - x)
            y = np.take_along_axis(B[q], hashes(w[q], z)[:, None, :], 2)
            n = M + L * t + lane
            X[r][:, :, M + L * t:M + L * t + L] = np.where(wb, x, 0)
            E[r][:, :, M + L * t:M + L * t + L] = np.where(wb & cap, c + 4096 * s, NONE)
            col = np.where(cap, NONE, ev); col[:, p, lane] = n[None, :] + 4096 * np.max(np.where(cap, s, 0), axis=1)
            gi, li = np.nonzero(win)
            E[r][gi, :, v[gi, li]] = col[gi, :, li]
            x = np.where(wb, np.abs(x - y), x)
            back = np.add.reduce(w[r][:, :, 0:1] * x, axis=1) & (R - 1)
            xs[r] = x; vs[r] = np.where(win, back, np.where(go, down, v))
    return {"ykids": E.reshape(N, 128, W).astype(np.float32), "ynodes": np.ascontiguousarray(X[..., M:]).reshape(N, 128, L * T).astype(np.float32).astype(BF),
            "ycand": xs.reshape(N, 128, L).astype(np.float32).astype(BF), "yspot": np.stack([gtable(a) for a in vs]).astype(np.float32)}

@@ -1,0 +1,583 @@
+import math
+from concourse.bass import DstId, RemoteDMATransfer
+from concourse.mybir import AluOpType as A, ActivationFunctionType as F
+
+N = 8
+M, L, NT = 2048, 192, 4
+W = M + L * NT
+BIGM = 1.5 * 2.0 ** 35
+LN32 = math.log(32.0)
+
+SCRATCH = {
+    "kI": ("sbuf", [128, 2048], "int32"), "Ef": ("sbuf", [128, 2816], "float32"),
+    "X": ("sbuf", [128, 4096], "bfloat16"), "bk3": ("sbuf", [128, 6144], "bfloat16"),
+    "x": ("sbuf", [128, 192], "bfloat16"), "sp": ("sbuf", [128, 12], "int32"), "wt": ("sbuf", [128, 2], "bfloat16"),
+    "ia": ("sbuf", [128, 192], "int32"), "ic": ("sbuf", [128, 192], "int32"), "ic2": ("sbuf", [128, 192], "int32"),
+    "ib": ("sbuf", [128, 128], "int32"), "dgi": ("sbuf", [128, 192], "int32"), "i8": ("sbuf", [128, 8], "int32"),
+    "p0": ("sbuf", [128, 1], "int32"), "p1": ("sbuf", [128, 1], "int32"), "p2": ("sbuf", [128, 1], "int32"),
+    "pm": ("sbuf", [128, 1], "float32"), "pb": ("sbuf", [128, 1], "float32"),
+    "nci": ("sbuf", [128, 768], "int32"), "NC": ("sbuf", [128, 768], "float16"),
+    "dli": ("sbuf", [128, 48], "int32"), "DL": ("sbuf", [128, 48], "float32"), "DLm": ("sbuf", [128, 48], "float32"),
+    "dgS": ("sbuf", [128, 192], "bfloat16"), "LT": ("sbuf", [128, 8, 16], "bfloat16"),
+    "NegI": ("sbuf", [128, 128], "bfloat16"), "NI4": ("sbuf", [128, 128], "bfloat16"),
+    "PI4": ("sbuf", [128, 128], "bfloat16"), "Idb": ("sbuf", [128, 128], "bfloat16"), "xc": ("sbuf", [128, 1024], "bfloat16"),
+    "Idh": ("sbuf", [128, 128], "float16"), "B16": ("sbuf", [128, 128], "bfloat16"),
+    "B16h": ("sbuf", [128, 128], "float16"), "B4h": ("sbuf", [128, 128], "float16"),
+    "BT": ("sbuf", [128, 128], "bfloat16"), "Tri": ("sbuf", [128, 128], "bfloat16"),
+    "tri0": ("sbuf", [128, 128], "bfloat16"), "G8": ("sbuf", [128, 8], "bfloat16"),
+    "Sm": ("sbuf", [128, 2048], "float16"), "RM": ("sbuf", [128, 192], "float32"),
+    "c88": ("sbuf", [128, 192], "float16"), "cneg": ("sbuf", [128, 128], "bfloat16"),
+    "cva": ("sbuf", [128, 1], "float32"), "cvb": ("sbuf", [128, 1], "float32"),
+    "cvc": ("sbuf", [128, 1], "float32"), "ones": ("sbuf", [128, 128], "bfloat16"),
+    "PW1": ("sbuf", [128, 143], "bfloat16"), "PW2": ("sbuf", [128, 143], "bfloat16"), "P1s": ("sbuf", [128, 143], "bfloat16"),
+    "voff": ("sbuf", [128, 12], "uint16"), "soff": ("sbuf", [128, 12], "uint16"), "vm": ("sbuf", [128, 12], "float32"),
+    "vp1": ("sbuf", [128, 12], "float32"), "vmh": ("sbuf", [128, 12], "float16"), "vmd": ("sbuf", [128, 12], "float32"),
+    "bki": ("sbuf", [128, 12], "int32"), "bka": ("sbuf", [128, 12], "int32"), "bkf": ("sbuf", [128, 12], "float32"),
+    "bmv": ("sbuf", [128, 12], "float32"), "vlw": ("sbuf", [128, 12], "float32"), "ta": ("sbuf", [128, 12], "float32"),
+    "tb": ("sbuf", [128, 12], "float32"), "tc": ("sbuf", [128, 12], "float32"), "ts": ("sbuf", [128, 12], "float32"),
+    "ts2": ("sbuf", [128, 12], "float32"), "vfin": ("sbuf", [128, 12], "float32"),
+    "ev": ("sbuf", [128, 192], "int32"), "Ci": ("sbuf", [128, 192], "int32"), "offs": ("sbuf", [128, 192], "uint16"),
+    "xr": ("sbuf", [128, 2048], "bfloat16"), "diff": ("sbuf", [128, 3072], "bfloat16"),
+    "D": ("sbuf", [128, 3072], "bfloat16"), "sg": ("sbuf", [128, 3072], "bfloat16"), "cmp": ("sbuf", [128, 3072], "bfloat16"),
+    "zd": ("sbuf", [128, 192], "bfloat16"), "z": ("sbuf", [128, 192], "bfloat16"),
+    "hb": ("sbuf", [128, 512], "float32"), "sb": ("sbuf", [128, 512], "float32"), "Idf": ("sbuf", [128, 128], "float32"), "t2": ("sbuf", [128, 512], "bfloat16"), "u1s": ("sbuf", [128, 256], "float32"),
+    "Pi": ("sbuf", [128, 256], "int32"), "Pd": ("sbuf", [128, 256], "int32"), "He": ("sbuf", [128, 256], "float32"),
+    "h": ("sbuf", [128, 192], "uint16"),
+    "Ki": ("sbuf", [128, 192], "int32"), "emp": ("sbuf", [128, 192], "bfloat16"), "edg": ("sbuf", [128, 192], "bfloat16"),
+    "K2": ("sbuf", [128, 192], "float32"), "Cf": ("sbuf", [128, 192], "float16"), "bigK": ("sbuf", [128, 192], "float32"),
+    "CN": ("sbuf", [128, 384], "bfloat16"), "WW": ("sbuf", [128, 384], "bfloat16"), "isb": ("sbuf", [128, 384], "bfloat16"),
+    "sel": ("sbuf", [128, 384], "bfloat16"), "pay": ("sbuf", [128, 384], "float16"),
+    "wdgw": ("sbuf", [128, 192], "bfloat16"), "gdg": ("sbuf", [128, 192], "float32"), "dn": ("sbuf", [128, 192], "float32"),
+    "sc1": ("sbuf", [128, 192], "float32"), "sc2": ("sbuf", [128, 192], "float32"), "sc3": ("sbuf", [128, 192], "float32"),
+    "cR": ("sbuf", [128, 192], "float32"), "val": ("sbuf", [128, 192], "float32"), "wdg": ("sbuf", [128, 192], "bfloat16"),
+    "q2": ("sbuf", [128, 192], "float32"), "capw": ("sbuf", [128, 192], "bfloat16"), "q3": ("sbuf", [128, 192], "float32"),
+    "EQ": ("sbuf", [128, 12, 192], "bfloat16"), "xy": ("sbuf", [128, 192], "bfloat16"), "xw": ("sbuf", [128, 192], "bfloat16"),
+    "dx": ("sbuf", [128, 192], "bfloat16"),
+    "U0": ("psum", [128, 512], "float32"), "U1": ("psum", [128, 512], "float32"), "O": ("psum", [128, 512], "float32"),
+    "S0": ("psum", [128, 512], "float32"), "S1": ("psum", [128, 512], "float32"), "TB": ("psum", [128, 512], "float32"),
+    "VP": ("psum", [128, 512], "float32"), "CB": ("psum", [128, 512], "float32"),
+}
+SCRATCH["FP"] = ("sbuf", [128, 8 * 144], "bfloat16")
+for _n, _w, _d in (("wf", 2, "bfloat16"), ("zq", 12, "uint16"), ("qi", 12, "uint16"), ("yo", 192, "bfloat16"), ("yi", 192, "bfloat16")):
+    SCRATCH[_n] = ("sbuf", [128, NT * _w], _d)
+PSUM = [n for n in SCRATCH if SCRATCH[n][0] == "psum"]
+NDMA = 16
+SEMAPHORES = ["sV", "sS", "sP", "sG", "lsem", "wa"] + ["qa%d" % t for t in range(NT)] + ["ra%d" % t for t in range(NT)] + ["d%d" % i for i in range(NDMA)]
+
+
+def tracker(g, T):
+    eng = {"V": g.vector, "S": g.scalar, "P": g.tensor, "G": g, "Y": g.sync}
+    know = {q: {} for q in eng}
+    cnt = {q: 0 for q in eng}
+    wr, rd, bank, used = {}, {}, {}, [0]
+
+    def waits(q, ops):
+        k = know[q]
+        ops = [o for o in ops if k.get(o[0], 0) < o[1]]
+        ops.sort(key=lambda o: -len(o[2]))
+        best = {}
+        for o in ops:
+            if o[0] not in best or best[o[0]][1] < o[1]:
+                best[o[0]] = o
+        ops = list(best.values())
+        keep = []
+        for o in ops:
+            if not any(p is not o and p[2].get(o[0], 0) >= o[1] for p in ops):
+                keep.append(o)
+        for o in keep:
+            eng[q].wait_ge(T.sem[o[0]], o[1])
+        for o in keep:
+            for s, v in o[2].items():
+                if k.get(s, 0) < v:
+                    k[s] = v
+
+    def deps(q, reads, writes, dma):
+        out = []
+        for n, lo, hi in reads:
+            out += [o for a, b, o in wr.get(n, []) if a < hi and lo < b]
+        for n, lo, hi in writes:
+            for a, b, o in wr.get(n, []):
+                if a < hi and lo < b and not (o[3] == q == "P"):
+                    out.append(o)
+            for a, b, o in rd.get(n, []):
+                if a < hi and lo < b and (o[3] != q or dma):
+                    out.append(o)
+        for n in set([r[0] for r in reads + writes]):
+            if n in PSUM:
+                out += [o for p, o in bank.get(n, {}).items() if p != q]
+        if q == "P":
+            out = [o for o in out if o[3] != "P"]
+        return out
+
+    def note(op, reads, writes, q):
+        for n, lo, hi in writes:
+            wr[n] = [e for e in wr.get(n, []) if not (lo <= e[0] and e[1] <= hi)] + [(lo, hi, op)]
+            rd[n] = [e for e in rd.get(n, []) if not (lo <= e[0] and e[1] <= hi)]
+        for n, lo, hi in reads:
+            old = [e for e in rd.get(n, []) if not (lo <= e[0] and e[1] <= hi and e[2][3] == q and op[4] == 0 and e[2][4] == 0)]
+            rd[n] = old + [(lo, hi, op)]
+        for n in set([r[0] for r in reads + writes]):
+            if n in PSUM:
+                bank.setdefault(n, {})[q] = op
+
+    def emit(q, call, reads, writes, dma=False):
+        waits(q, deps(q, reads, writes, dma))
+        ins = call(eng[q])
+        if dma:
+            s, v = "d%d" % used[0], 16
+            used[0] += 1
+        else:
+            cnt[q] += 1
+            s, v = "s" + q, cnt[q]
+        ins.then_inc(T.sem[s], 16 if dma else 1)
+        clk = dict(know[q])
+        clk[s] = v
+        note((s, v, clk, "d" if dma else q, 1 if dma else 0), reads, writes, q)
+
+    def arrive(sem, val, name, lo, hi):
+        note((sem, val, {sem: val}, "X", 1), [], [(name, lo, hi)], "X")
+
+    def before(q, reads):
+        waits(q, deps(q, reads, [], True))
+
+    def finish():
+        for q in eng:
+            if cnt[q]:
+                g.wait_ge(T.sem["s" + q], cnt[q])
+        for i in range(used[0]):
+            g.wait_ge(T.sem["d%d" % i], 16)
+    return emit, arrive, before, finish
+
+
+def rank_program(g, core, T, topo):
+    r = T.rank_of(core)
+    if r is None:
+        return
+    emit, arrive, before, finish = tracker(g, T)
+    width = {n: (SCRATCH[n][1][1] if len(SCRATCH[n][1]) == 2 else SCRATCH[n][1][1] * SCRATCH[n][1][2]) for n in SCRATCH}
+
+    def o(n, lo=0, hi=None, step=1):
+        hi = width[n] if hi is None else hi
+        return (T[n][:, lo:hi] if step == 1 else T[n][:, lo:hi:step], [(n, lo, hi)])
+
+    def ind(n, lo, hi, off):
+        return (T[n][:, lo:hi].indirect(off[0]), [(n, lo, hi)] + off[1])
+
+    def sca(s):
+        return (s[0], s[1]) if isinstance(s, tuple) else (s, [])
+
+    def tt(out, a, b, op):
+        emit("V", lambda e: e.tensor_tensor(out[0], a[0], b[0], op), a[1] + b[1], out[1])
+
+    def ts(out, a, s1, op0, s2=None, op1=None):
+        s1 = sca(s1)
+        if op1 is None:
+            emit("V", lambda e: e.tensor_scalar(out[0], a[0], s1[0], None, op0), a[1] + s1[1], out[1])
+        else:
+            emit("V", lambda e: e.tensor_scalar(out[0], a[0], s1[0], s2, op0, op1), a[1] + s1[1], out[1])
+
+    def cp(out, a):
+        emit("V", lambda e: e.tensor_copy(out[0], a[0]), a[1] + out[1][1:], out[1][:1])
+
+    def ms(out, c):
+        emit("V", lambda e: e.memset(out[0], c), [], out[1])
+
+    def scan(out, a, b):
+        emit("V", lambda e: e.tensor_tensor_scan(out[0], a[0], b[0], 0.0, A.mult, A.add), a[1] + b[1], out[1])
+
+    def act(out, a, func, scale=1.0, bias=0.0):
+        emit("S", lambda e: e.activation(out[0], a[0], func, bias=bias, scale=scale), a[1], out[1])
+
+    def mm(out, lhsT, rhs, start, stop):
+        emit("P", lambda e: e.matmul(out[0], lhsT[0], rhs[0], start, stop), lhsT[1] + rhs[1], out[1])
+
+    def iota(n, pattern, base, cm):
+        b = o(n)
+        emit("G", lambda e: e.iota(b[0], pattern, base, cm), [], b[1])
+
+    def load(q, name, lo, hi, src):
+        b = o(name, lo, hi)
+        emit(q, lambda e: e.dma_start(b[0], src), [], b[1], dma=True)
+
+    def store(q, dst, b):
+        emit(q, lambda e: e.dma_start(dst, b[0]), b[1], [], dma=True)
+
+    load("S", "wt", 0, 2, T.wts[:, :])
+    load("Y", "sp", 0, 12, T.spot[:, :])
+    load("Y", "kI", 0, 2048, T.kids[:, :])
+    load("S", "x", 0, 192, T.cand[:, :])
+    load("Y", "X", 0, 2048, T.nodes[:, :])
+    for j in range(3):
+        load("Y", "bk3", 2048 * j, 2048 * j + 2048, T.book[:, :])
+
+    iota("p0", [[0, 1]], 0, 1)
+    iota("ia", [[1, 192]], 1024, -1)
+    iota("ic", [[1, 192]], 0, 0)
+    iota("i8", [[1, 8]], 0, 0)
+    iota("dli", [[16, 48]], 2048, 0)
+    iota("nci", [[1, 768]], -2047, 0)
+
+    allto = [T.cores[(r - 1 - t) % N] for t in range(NT)]
+    common = [e for e in topo.engines(core, allto[0]) if all(e in topo.engines(core, c) for c in allto)][:8]
+    wmask = sum(1 << e for e in common)
+    lcount = [0]
+    before("G", [("wt", 0, 2)])
+    g.remote_dma_fused([RemoteDMATransfer(
+        dst_ids=[DstId(rid=topo.addr(c)[0], pnc=topo.addr(c)[1]) for c in allto], dma_engine_mask=wmask,
+        remote_sem=T.sem.wa, srcs=[T.wt[:, :]], dsts=[T.wf[:, 2 * t:2 * t + 2] for t in range(NT)])], local_sem=T.sem.lsem)
+    lcount[0] += len(common)
+    for t in range(NT):
+        arrive("wa", len(common) * NT, "wf", 2 * t, 2 * t + 2)
+
+    def send(dst, out_n, in_n, lo, hi, sem):
+        eng = topo.engines(core, dst)[:8]
+        before("G", [(in_n, lo, hi)])
+        rid, pid, _s = topo.addr(dst)
+        g.remote_dma(T[out_n][:, lo:hi], T[in_n][:, lo:hi], T.sem[sem], T.sem.lsem, pid, rid, sum(1 << e for e in eng))
+        lcount[0] += len(eng)
+
+    ms(o("X", 2048, 4080), 0.0)
+    ms(o("X", 4080, 4096), 512.0)
+    ms(o("Ef", 2048, 2816), 4095.0)
+    for n in ("PW1", "PW2", "P1s", "FP"):
+        ms(o(n), 0.0)
+    ms(o("ones"), 1.0)
+    cp(o("voff"), o("sp"))
+    ts(o("vm"), o("sp"), -1408.0, A.add)
+    ts(o("vp1"), o("sp"), 1.0, A.add)
+    cp(o("vmh"), o("vm"))
+    ts(o("p1"), o("p0"), 15, A.bitwise_and)
+    cp(o("pm"), o("p1"))
+    ts(o("p2"), o("p0"), 4, A.arith_shift_right)
+    cp(o("pb"), o("p2"))
+    ts(o("dgi"), o("ia"), 15, A.bitwise_and)
+    ts(o("dgS"), o("dgi"), 0.0, A.is_equal)
+    dgP = lambda lo, hi: o("VP", lo, hi)
+    ts(o("VP", 0, 192), o("dgi"), 0.0, A.is_equal)
+    ts(o("NegI"), o("ia", 0, 128), 1024.0, A.is_equal, -1.0, A.mult)
+    ts(o("NI4"), o("ia", 0, 128), 1024.0, A.is_equal, -1.0 / 4096, A.mult)
+    ts(o("PI4"), o("ia", 0, 128), 1024.0, A.is_equal, 1.0 / 4096, A.mult)
+    ts(o("Idb"), o("ia", 0, 128), 1024.0, A.is_equal)
+    ts(o("Idf"), o("ia", 0, 128), 1024.0, A.is_equal)
+    ts(o("Idh"), o("ia", 0, 128), 1024.0, A.is_equal)
+    ts(o("ib"), o("ic", 0, 128), 4, A.arith_shift_right)
+    ts(o("B16"), o("ib"), o("pb"), A.is_equal)
+    cp(o("B16h"), o("B16"))
+    ts(o("B4h"), o("B16"), 4096.0, A.mult)
+    ts(o("BT"), o("B16"), 3.0 / 64, A.mult)
+    ts(o("tri0"), o("ia", 0, 128), 1024.0, A.is_gt)
+    tt(o("Tri"), o("tri0"), o("B16"), A.mult)
+    ts(o("G8"), o("i8"), o("pb"), A.is_equal)
+    ts(o("P1s", 15, 143, 16), o("G8"), 1.0, A.mult)
+    ts(o("ic2"), o("ic"), 15, A.bitwise_and)
+    ts(o("RM"), o("ic2"), 0.0, A.is_gt)
+    for e_ in range(8):
+        ts((T.LT[:, e_, :], [("LT", 16 * e_, 16 * e_ + 16)]), o("ic", 0, 16), o("pm"), A.is_gt)
+    ts(o("cva"), o("dgS", 0, 1), -2048.0, A.mult)
+    ts(o("cvb"), o("dgS", 1, 2), 0.5, A.mult)
+    tt(o("cvc"), o("cva"), o("cvb"), A.add)
+    ts(o("cneg"), o("ones"), o("cvc"), A.mult)
+    ts(o("c88"), o("RM"), 0.0, A.mult, 88.0625, A.add)
+    for m in range(16):
+        ts(o("Sm", 128 * m, 128 * m + 128), o("B16h"), o("dgS", m, m + 1), A.mult)
+    ts(o("DL"), o("dli"), o("pm"), A.add)
+    ts(o("DLm"), o("DL"), -1408.0, A.add)
+    cp(o("NC"), o("nci"))
+    ts(o("PW1", 15, 143, 16), o("G8"), o("wt", 0, 1), A.mult)
+    ts(o("PW2", 15, 143, 16), o("G8"), o("wt", 1, 2), A.mult)
+
+    def window(n, k, base=0):
+        return o(n, base + 15 - k, base + 143 - k)
+
+    def repeat():
+        for k in range(16):
+            act((T.xr[:, k:2048:16], [("xr%d" % k, 0, 2048)]), o("x", 0, 128), F.Copy)
+
+    repeat()
+
+    CH = ((0, 64), (64, 128), (128, 192))
+    UB = ("U0", "U1", "U0")
+    deferred = []
+
+    def gather_slots(t, lo, hi):
+        tab = ("kI", 0, 2048) if t == 0 else ("Ef", 0, W)
+        cp(o("ev", lo, hi), ind(tab[0], tab[1], tab[2], o("voff", lo // 16, hi // 16)))
+        ts(o("Ci", lo, hi), o("ev", lo, hi), 4095, A.bitwise_and)
+        cp(o("offs", lo, hi), o("Ci", lo, hi))
+
+    def hash_mod(U, n, w):
+        act(o("hb", 128 * w, 128 * w + 2 * n), o(U, 0, 2 * n), F.Identity, bias=BIGM)
+        act(o("sb", 128 * w, 128 * w + 2 * n), o(U, 0, 2 * n), F.Identity, bias=2047.5)
+        act(o("t2", 128 * w, 128 * w + 2 * n), o("hb", 128 * w, 128 * w + 2 * n), F.Identity, bias=-BIGM)
+        mm(o(U, 256, 256 + 2 * n), o("Idf"), o("sb", 128 * w, 128 * w + 2 * n), True, False)
+        mm(o(U, 256, 256 + 2 * n), o("NegI"), o("t2", 128 * w, 128 * w + 2 * n), False, True)
+        act(o("u1s", 64 * w, 64 * w + n), o(U, 256, 256 + n), F.Copy)
+
+    def hash_end(U, n, w, out):
+        c = (64 * w, 64 * w + n)
+        u2 = o(U, 256 + n, 256 + 2 * n)
+        tt(o("Pi", *c), o("u1s", *c), u2, A.mult)
+        ts(o("Pd", *c), o("Pi", *c), 5, A.arith_shift_right, 2047, A.bitwise_and)
+        tt(o("He", *c), o("Pd", *c), u2, A.add)
+        cp(out, o("He", *c))
+
+    for t in range(NT):
+        last = t == NT - 1
+        b = T.cores[(r + 1 + t) % N]
+        asker = T.cores[(r - 1 - t) % N]
+
+        def XG(c):
+            lo, hi = CH[c]
+            dv = o("diff", 16 * lo, 16 * hi)
+            xg = ind("X", 0, 4096, o("offs", lo, hi))
+            xv = (T.xr[:, 16 * lo:16 * hi], [("xr%d" % k, 16 * lo, 16 * hi) for k in range(16)])
+            tt(dv, xg, xv, A.subtract)
+            act(o("D", 16 * lo, 16 * hi), dv, F.Abs)
+
+        def usum(c, j):
+            lo, hi = CH[c]
+            U = UB[c]
+            if j == 0:
+                mm(o(U, 0, 128), o("B16"), o("cneg"), True, False)
+            for k in range(16):
+                mm(o(U, 64 * j, 64 * j + 64), window("PW%d" % (j + 1), k), o("D", 16 * lo + k, 16 * hi, 16), False, j == 1 and k == 15)
+
+        def BG(c):
+            lo, hi = CH[c]
+            tt(o("cmp", 16 * lo, 16 * hi), ind("bk3", 0, 6144, o("h", lo, hi)), o("D", 16 * lo, 16 * hi), A.is_ge)
+
+        def sign(c):
+            lo, hi = CH[c]
+            if c == 2:
+                for hf in range(2):
+                    act(o("sg", 2048 + 512 * hf, 2560 + 512 * hf), o(("TB", "S1")[hf]), F.Sign, scale=-1.0, bias=0.5)
+            else:
+                ts(o("sg", 16 * lo, 16 * hi), o("diff", 16 * lo, 16 * hi), 0.0, A.is_le)
+
+        def over(c):
+            lo, hi = CH[c]
+            for k in range(16):
+                mm(o("O", lo, hi), window("P1s", k), o("sg", 16 * lo + k, 16 * hi, 16), k == 0, k == 15)
+
+        def ssum(c):
+            lo, hi = CH[c]
+            so = o("S0", lo, hi) if c < 2 else o("S1", 0, 64)
+            mm(so, o("PI4"), o("emp", lo, hi), True, False)
+            mm(so, o("NI4"), o("edg", lo, hi), False, False)
+            for k in range(16):
+                mm(so, window("P1s", k), o("cmp", 16 * lo + k, 16 * hi, 16), False, k == 15)
+
+        gather_slots(t, 0, 64)
+        if t == 0:
+            gather_slots(t, 64, 192)
+            cp(o("Ef", 0, 2048), o("kI"))
+            for j in range(2 * NT):
+                ts(o("FP", 144 * j + 15, 144 * j + 143, 16), o("G8"), o("wf", j, j + 1), A.mult)
+        tt(o("zd"), ind("X", 0, 4096, o("voff")), o("x"), A.subtract)
+        act(o("z"), o("zd"), F.Abs)
+        if t > 0:
+            gather_slots(t, 64, 192)
+        act(o("xc"), ind("X", 0, 4096, o("offs", 128, 192)), F.Copy)
+        mm(o("U1", 0, 24), o("B16"), o("cneg", 0, 24), True, False)
+        for j in range(2):
+            for m in range(16):
+                mm(o("U1", 12 * j, 12 * j + 12), window("FP", m, 144 * (2 * t + j)), o("z", m, 192, 16), False, j == 1 and m == 15)
+        XG(0)
+        for f in deferred:
+            f()
+        del deferred[:]
+        usum(0, 0)
+        hash_mod("U1", 12, 3)
+        usum(0, 1)
+        XG(1)
+        ts(o("emp"), o("Ci"), 4095.0, A.is_equal, -4096.0, A.mult)
+        ts(o("Ki"), o("ev"), 12, A.arith_shift_right)
+        hash_end("U1", 12, 3, o("zq", 12 * t, 12 * t + 12))
+        send(b, "qi", "zq", 12 * t, 12 * t + 12, "qa%d" % t)
+        arrive("qa%d" % t, len(topo.engines(asker, core)[:8]), "qi", 12 * t, 12 * t + 12)
+        arrive("ra%d" % t, len(topo.engines(b, core)[:8]), "yi", L * t, L * t + L)
+        for hf in range(2):
+            bank = ("TB", "S1")[hf]
+            mm(o(bank), o("Idb"), o("xc", 512 * hf, 512 * hf + 512), True, False)
+            for k in range(16):
+                mm(o(bank, k, 512, 16), o("NegI"), o("x", 128 + 32 * hf, 160 + 32 * hf), False, k == 15)
+        hash_mod("U0", 64, 0)
+        for hf in range(2):
+            act(o("D", 2048 + 512 * hf, 2560 + 512 * hf), o(("TB", "S1")[hf]), F.Abs)
+        usum(1, 0)
+        usum(1, 1)
+        sign(0)
+        tt(o("edg"), dgP(0, 192), o("emp"), A.mult)
+        ts(o("Cf"), o("Ci"), -1408.0, A.add)
+        tt(o("K2"), o("Ki"), o("edg"), A.add)
+        hash_end("U0", 64, 0, o("h", 0, 64))
+        BG(0)
+        hash_mod("U1", 64, 1)
+        usum(2, 0)
+        usum(2, 1)
+        sign(2)
+        ts(o("VP", 256, 448), o("ev"), -1.0, A.mult, 4095.0, A.add)
+        hash_end("U1", 64, 1, o("h", 64, 128))
+        BG(1)
+        mm(o("CB", 0, 192), o("B16h"), o("c88"), True, False)
+        for m in range(16):
+            mm(o("CB", m, 192, 16), o("Sm", 128 * m, 128 * m + 128), o("vmh"), False, m == 15)
+        over(0)
+        hash_mod("U0", 64, 2)
+        ssum(0)
+        sign(1)
+        over(1)
+        act(o("yo", L * t, L * t + L), ind("bk3", 0, 6144, o("qi", 12 * t, 12 * t + 12)), F.Copy)
+        send(asker, "yi", "yo", L * t, L * t + L, "ra%d" % t)
+        act(o("O", 192, 320), o("O", 0, 128), F.Relu, scale=-128.0, bias=1216.0)
+        hash_end("U0", 64, 2, o("h", 128, 192))
+        BG(2)
+        ssum(1)
+        tt(o("vmd"), o("vm"), o("DLm", 12 * t, 12 * t + 12), A.subtract)
+
+        def batch(lo, hi, SB, t=t, last=last):
+            n = hi - lo
+            c0, c1 = lo // 16, hi // 16
+            a, e = 2 * lo, 2 * lo + n
+            z_ = 2 * hi
+            T0, L0, W0 = (0, 256, 256) if lo == 0 else (384, 384, 0)
+            S = o(SB, 0, n)
+            EX = o(SB, n, 2 * n)
+            Q1 = o(SB, 2 * n, 3 * n)
+            last_lane = lambda nm: o(nm, lo + 15, hi, 16)
+            lst = lambda nm: o(nm, c0, c1)
+
+            def d1():
+                act(EX, S, F.Exp, scale=LN32)
+                act(Q1, S, F.Identity, scale=4096.0, bias=-4095.0)
+                tt(o("bigK", lo, hi), o("O", 192 + lo, 192 + hi), o("K2", lo, hi), A.add)
+                tt(o("CN", e, z_), S, o("bigK", lo, hi), A.is_gt)
+                tt(o("CN", a, e), S, o("bigK", lo, hi), A.is_le)
+                tt(o("WW", a, e), EX, o("CN", a, e), A.mult)
+                tt(o("WW", e, z_), EX, o("CN", e, z_), A.mult)
+                mm(o("TB", T0, T0 + 2 * n), o("BT"), o("WW", a, z_), True, True)
+
+            def d2():
+                tt(o("wdgw", lo, hi), dgP(lo, hi), o("CN", e, z_), A.mult)
+                scan(o("sc1", lo, hi), o("RM", lo, hi), o("wdgw", lo, hi))
+                tt(o("isb", a, z_), o("WW", a, z_), o("TB", T0, T0 + 2 * n), A.is_gt)
+                mm(o("TB", L0, L0 + 2 * n), o("Tri"), o("isb", a, z_), True, True)
+
+            def d3():
+                tt(lst("vlw"), last_lane("sc1"), lst("vp1"), A.mult)
+                tt(o("gdg", lo, hi), dgP(lo, hi), o("CN", a, e), A.mult)
+                tt(Q1, Q1, o("Ci", lo, hi), A.add)
+                tt(o("sel", a, z_), o("isb", a, z_), o("TB", L0, L0 + 2 * n), A.is_gt)
+                tt(o("pay", e, z_), S, o("sel", e, z_), A.mult)
+                tt(o("pay", a, e), o("sel", a, e), o("Cf", lo, hi), A.mult)
+                mm(o("TB", T0 + n, T0 + 2 * n), o("Idh"), o("NC", L * t + lo, L * t + hi), True, False)
+                mm(o("TB", T0 + n, T0 + 2 * n), o("B4h"), o("pay", e, z_), False, True)
+                mm(o("TB", T0, T0 + n), o("B16h"), o("pay", a, e), True, True)
+
+            def d4():
+                for c in range(c0, c1):
+                    ts((T.EQ[:, c, 0:L - 16 * c], [("EQ", L * c, L * c + L - 16 * c)]), o("CB", 16 * c, L), o("vlw", c, c + 1), A.is_equal)
+                eqd = (T.EQ[:, c0:c1, 0:16], [("EQ", L * c0, L * c1)])
+                tt(eqd, eqd, (T.LT[:, 0:c1 - c0, :], [("LT", 0, 16 * (c1 - c0))]), A.mult)
+
+                def count(cs, x0, x1, first, final):
+                    for c in cs:
+                        s = max(x0, 16 * c)
+                        mm(o("CB", 192 + s, 192 + x1), o("B16"), (T.EQ[:, c, s - 16 * c:x1 - 16 * c], [("EQ", L * c, L * c + L)]),
+                           first and c == cs[0], final and c == cs[-1])
+                if lo == 0:
+                    count(list(range(8)), 0, 128, True, True)
+                else:
+                    count(list(range(12)), 128, 192, True, True)
+
+            def d5():
+                tt(o("VP", 256 + lo, 256 + hi), o("VP", 256 + lo, 256 + hi), o("CN", e, z_), A.mult)
+                tt(o("VP", 256 + lo, 256 + hi), o("VP", 256 + lo, 256 + hi), o("ev", lo, hi), A.add)
+                tt(o("wdg", lo, hi), o("wdgw", lo, hi), o("CB", 192 + lo, 192 + hi), A.is_gt)
+                mm(o("TB", W0, W0 + n), o("B16"), o("wdg", lo, hi), True, True)
+                scan(o("sc3", lo, hi), o("RM", lo, hi), o("wdg", lo, hi))
+                tt(lst("ts"), last_lane("sc3"), lst("vmd"), A.mult)
+                tt(o("dn", lo, hi), o("TB", T0, T0 + n), o("gdg", lo, hi), A.mult)
+                tt(lst("ts2"), lst("ts"), o("DL", 12 * t + c0, 12 * t + c1), A.add)
+                tt(o("cR", lo, hi), o("TB", T0 + n, T0 + 2 * n), o("dgS", lo, hi), A.mult)
+                cp(lst("soff"), lst("ts2"))
+                scan(o("sc2", lo, hi), o("RM", lo, hi), o("dn", lo, hi))
+                tt(o("val", lo, hi), o("VP", 256 + lo, 256 + hi), o("cR", lo, hi), A.add)
+                tt(lst("ta"), last_lane("sc1"), lst("vm"), A.mult)
+                cp(ind("Ef", 0, W, lst("soff")), o("val", lo, hi))
+                tt(lst("tb"), lst("ta"), last_lane("sc2"), A.add)
+
+            def d8():
+                tt(lst("tc"), last_lane("sc3"), lst("bmv"), A.mult)
+                tt(lst("vm"), lst("tb"), lst("tc"), A.add)
+                if last:
+                    ts(lst("vfin"), lst("vm"), 1408.0, A.add)
+                else:
+                    ts(lst("voff"), lst("vm"), 1408.0, A.add)
+
+            def d6():
+                WR = o("TB", W0, W0 + n)
+                nl = M + L * t
+                tt(o("VP", 256 + lo, 256 + hi), WR, o("dx", lo, hi), A.mult)
+                tt(o("X", nl + lo, nl + hi), WR, o("x", lo, hi), A.mult)
+                tt(o("x", lo, hi), o("VP", 256 + lo, 256 + hi), o("x", lo, hi), A.add)
+                if not last and lo == 0:
+                    repeat()
+
+            def d7():
+                nl = M + L * t
+                tt(o("capw", lo, hi), o("TB", W0, W0 + n), o("CN", e, z_), A.mult)
+                tt(o("q3", lo, hi), Q1, o("capw", lo, hi), A.mult)
+                act(o("Ef", nl + lo, nl + hi), o("q3", lo, hi), F.Identity, bias=4095.0)
+
+            def d9():
+                cp(lst("vmh"), lst("vm"))
+                ts(lst("vp1"), lst("vm"), 1409.0, A.add)
+            return d1, d2, d3, d4, d5, d6, d7, d8, d9
+
+        AB = batch(0, 128, "S0")
+        C = batch(128, 192, "S1")
+        ssum(2)
+        AB[0]()
+        over(2)
+        act(o("O", 320, 384), o("O", 128, 192), F.Relu, scale=-64.0, bias=192.0)
+        AB[1]()
+        AB[2]()
+        C[0]()
+        mm(o("O", 0, 192), o("Idb"), o("x"), True, False)
+        mm(o("O", 0, 192), o("NegI"), o("yi", L * t, L * t + L), False, True)
+        act(o("xw"), o("O", 0, 192), F.Abs)
+        AB[3]()
+        C[1]()
+        mm(o("O", 0, 192), o("Idb"), o("xw"), True, False)
+        mm(o("O", 0, 192), o("NegI"), o("x"), False, True)
+        act(o("dx"), o("O", 0, 192), F.Copy)
+        for m in range(16):
+            mm(o("O", 384, 396), window("PW1", m), o("xw", m, 192, 16), m == 0, m == 15)
+        C[2]()
+        AB[4]()
+        cp(o("bki"), o("O", 384, 396))
+        ts(o("bka"), o("bki"), 1023, A.bitwise_and)
+        C[3]()
+        ts(o("bkf"), o("bka"), 1.0, A.add)
+        AB[6]()
+        tt(o("bmv"), o("bkf"), o("vp1"), A.subtract)
+        AB[5]()
+        AB[7]()
+        C[4]()
+        C[7]()
+        C[5]()
+        if not last:
+            AB[8]()
+        if last:
+            store("Y", T.ykids[:, 0:W - L], o("Ef", 0, W - L))
+            C[6]()
+            store("S", T.ykids[:, W - L:W], o("Ef", W - L, W))
+            store("Y", T.ynodes[:, :], o("X", M, W))
+            store("S", T.ycand[:, :], o("x"))
+            store("Y", T.yspot[:, :], o("vfin"))
+        else:
+            deferred.extend((C[8], C[6]))
+
+    finish()
+    g.wait_ge(T.sem.lsem, lcount[0])

@@ -26,9 +26,7 @@ SCRATCH = {
     "BT": ("sbuf", [128, 128], "bfloat16"), "Tri": ("sbuf", [128, 128], "bfloat16"),
     "tri0": ("sbuf", [128, 128], "bfloat16"), "G8": ("sbuf", [128, 8], "bfloat16"),
     "Sm": ("sbuf", [128, 2048], "float16"), "RM": ("sbuf", [128, 192], "float32"),
-    "c88": ("sbuf", [128, 192], "float16"), "cneg": ("sbuf", [128, 128], "bfloat16"),
-    "cva": ("sbuf", [128, 1], "float32"), "cvb": ("sbuf", [128, 1], "float32"),
-    "cvc": ("sbuf", [128, 1], "float32"), "ones": ("sbuf", [128, 128], "bfloat16"),
+    "c88": ("sbuf", [128, 192], "float16"),
     "PW1": ("sbuf", [128, 143], "bfloat16"), "PW2": ("sbuf", [128, 143], "bfloat16"), "P1s": ("sbuf", [128, 143], "bfloat16"),
     "voff": ("sbuf", [128, 12], "uint16"), "soff": ("sbuf", [128, 12], "uint16"), "vm": ("sbuf", [128, 12], "float32"),
     "vp1": ("sbuf", [128, 12], "float32"), "vmh": ("sbuf", [128, 12], "float16"), "vmd": ("sbuf", [128, 12], "float32"),
@@ -40,7 +38,7 @@ SCRATCH = {
     "xr": ("sbuf", [128, 2048], "bfloat16"), "diff": ("sbuf", [128, 3072], "bfloat16"),
     "D": ("sbuf", [128, 3072], "bfloat16"), "sg": ("sbuf", [128, 3072], "bfloat16"), "cmp": ("sbuf", [128, 3072], "bfloat16"),
     "zd": ("sbuf", [128, 192], "bfloat16"), "z": ("sbuf", [128, 192], "bfloat16"),
-    "hb": ("sbuf", [128, 512], "float32"), "sb": ("sbuf", [128, 512], "float32"), "Idf": ("sbuf", [128, 128], "float32"), "t2": ("sbuf", [128, 512], "bfloat16"), "u1s": ("sbuf", [128, 256], "float32"),
+    "hb": ("sbuf", [128, 512], "float32"), "sb": ("sbuf", [128, 512], "float32"), "t2": ("sbuf", [128, 512], "bfloat16"), "u1s": ("sbuf", [128, 256], "float32"),
     "Pi": ("sbuf", [128, 256], "int32"), "Pd": ("sbuf", [128, 256], "int32"), "He": ("sbuf", [128, 256], "float32"),
     "h": ("sbuf", [128, 192], "uint16"),
     "Ki": ("sbuf", [128, 192], "int32"), "emp": ("sbuf", [128, 192], "bfloat16"), "edg": ("sbuf", [128, 192], "bfloat16"),
@@ -149,58 +147,166 @@ def tracker(g, T):
     return emit, arrive, before, finish
 
 
+WAKE, SELF = 0.10, 0.10
+
+
+def schedule(plan):
+    n = len(plan)
+    pred = [{} for _ in range(n)]
+    succ = [{} for _ in range(n)]
+    wr, rd = {}, {}
+
+    def edge(a, b, lat):
+        if a != b and pred[b].get(a, -1.0) < lat:
+            pred[b][a] = lat
+            succ[a][b] = lat
+    for i, (q, _c, reads, writes, kind, _d, after) in enumerate(plan):
+        for j in after:
+            edge(j, i, 0.0)
+        for b, lo, hi in reads:
+            for x, y, j in wr.get(b, []):
+                if x < hi and lo < y:
+                    edge(j, i, WAKE if plan[j][0] != q or kind == "d" else 0.0 if q == "P" else SELF)
+        for b, lo, hi in writes:
+            for x, y, j in wr.get(b, []) + rd.get(b, []):
+                if x < hi and lo < y:
+                    edge(j, i, WAKE if plan[j][0] != q else 0.0)
+        for b, lo, hi in writes:
+            wr[b] = [e for e in wr.get(b, []) if not (lo <= e[0] and e[1] <= hi)] + [(lo, hi, i)]
+            rd[b] = [e for e in rd.get(b, []) if not (lo <= e[0] and e[1] <= hi)]
+        for b, lo, hi in reads:
+            rd.setdefault(b, []).append((lo, hi, i))
+    left = [len(p) for p in pred]
+    end = [0.0] * n
+    early = [0.0] * n
+    free, bank, dfree = {}, {}, 0.0
+    banks = [sorted(set(b for b, _l, _h in p[2] + p[3] if b in PSUM)) for p in plan]
+    ready = [i for i in range(n) if left[i] == 0]
+    order = []
+    while ready:
+        best = None
+        for i in ready:
+            q = plan[i][0]
+            t = max(early[i], free.get(q, 0.0)) if q != "X" else early[i]
+            for b in banks[i]:
+                for q2, e in bank.get(b, {}).items():
+                    if q2 != q and e + WAKE > t:
+                        t = e + WAKE
+            key = (round(t / SLOT), i)
+            if best is None or key < best[0]:
+                best = (key, i, t)
+        _k, i, t = best
+        ready.remove(i)
+        order.append(i)
+        q, kind, d = plan[i][0], plan[i][4], plan[i][5]
+        if kind == "d":
+            free[q] = t + 0.1
+            dfree = max(dfree, t + 1.0) + d
+            end[i] = dfree + 1.0
+        else:
+            end[i] = t + d
+            free[q] = end[i]
+        for b in banks[i]:
+            bank.setdefault(b, {})[q] = end[i]
+        for j, lat in succ[i].items():
+            early[j] = max(early[j], end[i] + lat)
+            left[j] -= 1
+            if left[j] == 0:
+                ready.append(j)
+    return order
+
+
+SLOT = 0.02
+ORDER = {}
+
+
 def rank_program(g, core, T, topo):
     r = T.rank_of(core)
     if r is None:
         return
-    emit, arrive, before, finish = tracker(g, T)
+    emit_now, arrive_now, before, finish = tracker(g, T)
+    plan = []
+
+    def emit(q, call, reads, writes, dma=False, dur=0.06):
+        plan.append((q, [call], reads, writes, "d" if dma else "c", dur, []))
+
+    def cols(x):
+        return x[2] if len(x) > 2 else x[1][0][2] - x[1][0][1]
+
+    def dt_of(x):
+        return SCRATCH.get(x[1][0][0], ("sbuf", 0, "bfloat16"))[2]
+
+    def in_psum(x):
+        return x[1][0][0] in PSUM
+
+    CYC = 0.00085
+
+    def time_of(out, a, b=None):
+        if len(a) > 3:
+            return 0.06 + 1.56 * CYC * cols(out)
+        if len(out) > 3:
+            return 0.06 + 3.8 * CYC * cols(a)
+        n = cols(out)
+        if b is not None:
+            f = 1.0 if in_psum(a) or in_psum(b) else 2.0
+        else:
+            f = 0.5 if not in_psum(a) and not in_psum(out) and dt_of(a) in TWO and dt_of(out) in TWO else 1.0
+        return CYC * max(64, f * n)
+    TWO = ("bfloat16", "float16", "uint16")
+    group = []
     width = {n: (SCRATCH[n][1][1] if len(SCRATCH[n][1]) == 2 else SCRATCH[n][1][1] * SCRATCH[n][1][2]) for n in SCRATCH}
 
     def o(n, lo=0, hi=None, step=1):
         hi = width[n] if hi is None else hi
-        return (T[n][:, lo:hi] if step == 1 else T[n][:, lo:hi:step], [(n, lo, hi)])
+        return (T[n][:, lo:hi] if step == 1 else T[n][:, lo:hi:step], [(n, lo, hi)], (hi - lo + step - 1) // step)
 
     def ind(n, lo, hi, off):
-        return (T[n][:, lo:hi].indirect(off[0]), [(n, lo, hi)] + off[1])
+        return (T[n][:, lo:hi].indirect(off[0]), [(n, lo, hi)] + off[1], 16 * off[2], "indirect")
 
     def sca(s):
         return (s[0], s[1]) if isinstance(s, tuple) else (s, [])
 
     def tt(out, a, b, op):
-        emit("V", lambda e: e.tensor_tensor(out[0], a[0], b[0], op), a[1] + b[1], out[1])
+        emit("V", lambda e: e.tensor_tensor(out[0], a[0], b[0], op), a[1] + b[1], out[1], dur=time_of(out, a, b))
 
     def ts(out, a, s1, op0, s2=None, op1=None):
         s1 = sca(s1)
         if op1 is None:
-            emit("V", lambda e: e.tensor_scalar(out[0], a[0], s1[0], None, op0), a[1] + s1[1], out[1])
+            emit("V", lambda e: e.tensor_scalar(out[0], a[0], s1[0], None, op0), a[1] + s1[1], out[1], dur=time_of(out, a))
         else:
-            emit("V", lambda e: e.tensor_scalar(out[0], a[0], s1[0], s2, op0, op1), a[1] + s1[1], out[1])
+            emit("V", lambda e: e.tensor_scalar(out[0], a[0], s1[0], s2, op0, op1), a[1] + s1[1], out[1], dur=time_of(out, a))
 
     def cp(out, a):
-        emit("V", lambda e: e.tensor_copy(out[0], a[0]), a[1] + out[1][1:], out[1][:1])
+        emit("V", lambda e: e.tensor_copy(out[0], a[0]), a[1] + out[1][1:], out[1][:1], dur=time_of(out, a))
 
     def ms(out, c):
-        emit("V", lambda e: e.memset(out[0], c), [], out[1])
+        emit("V", lambda e: e.memset(out[0], c), [], out[1], dur=CYC * cols(out))
 
     def scan(out, a, b):
-        emit("V", lambda e: e.tensor_tensor_scan(out[0], a[0], b[0], 0.0, A.mult, A.add), a[1] + b[1], out[1])
+        emit("V", lambda e: e.tensor_tensor_scan(out[0], a[0], b[0], 0.0, A.mult, A.add), a[1] + b[1], out[1], dur=CYC * cols(out))
 
     def act(out, a, func, scale=1.0, bias=0.0):
-        emit("S", lambda e: e.activation(out[0], a[0], func, bias=bias, scale=scale), a[1], out[1])
+        emit("S", lambda e: e.activation(out[0], a[0], func, bias=bias, scale=scale), a[1], out[1],
+             dur=0.065 + CYC * cols(a) * (1.56 if len(a) > 3 else 1.0))
 
-    def mm(out, lhsT, rhs, start, stop):
-        emit("P", lambda e: e.matmul(out[0], lhsT[0], rhs[0], start, stop), lhsT[1] + rhs[1], out[1])
+    def mm(out, lhsT, rhs, start, stop, whole=None, cut=False):
+        group.append((lambda e: e.matmul(out[0], lhsT[0], rhs[0], start, stop), lhsT[1] + rhs[1], out[1] + ([(whole, 0, 512)] if whole else []),
+                      0.0007 * max(64, cols(rhs)) * (4 if dt_of(rhs) == "float32" else 1)))
+        if stop or cut:
+            plan.append(("P", [c[0] for c in group], sorted(set(x for c in group for x in c[1])), sorted(set(x for c in group for x in c[2])),
+                         "c", sum(c[3] for c in group), []))
+            del group[:]
 
     def iota(n, pattern, base, cm):
         b = o(n)
-        emit("G", lambda e: e.iota(b[0], pattern, base, cm), [], b[1])
+        emit("G", lambda e: e.iota(b[0], pattern, base, cm), [], b[1], dur=0.15 + 2 * CYC * cols(b))
 
     def load(q, name, lo, hi, src):
         b = o(name, lo, hi)
-        emit(q, lambda e: e.dma_start(b[0], src), [], b[1], dma=True)
+        emit(q, lambda e: e.dma_start(b[0], src), [], b[1], dma=True, dur=0.0013 * cols(b) * (1 if dt_of(b) in TWO else 2))
 
     def store(q, dst, b):
-        emit(q, lambda e: e.dma_start(dst, b[0]), b[1], [], dma=True)
+        emit(q, lambda e: e.dma_start(dst, b[0]), b[1], [], dma=True, dur=0.0013 * cols(b) * (1 if dt_of(b) in TWO else 2))
 
     load("S", "wt", 0, 2, T.wts[:, :])
     load("Y", "sp", 0, 12, T.spot[:, :])
@@ -221,27 +327,35 @@ def rank_program(g, core, T, topo):
     common = [e for e in topo.engines(core, allto[0]) if all(e in topo.engines(core, c) for c in allto)][:8]
     wmask = sum(1 << e for e in common)
     lcount = [0]
-    before("G", [("wt", 0, 2)])
-    g.remote_dma_fused([RemoteDMATransfer(
-        dst_ids=[DstId(rid=topo.addr(c)[0], pnc=topo.addr(c)[1]) for c in allto], dma_engine_mask=wmask,
-        remote_sem=T.sem.wa, srcs=[T.wt[:, :]], dsts=[T.wf[:, 2 * t:2 * t + 2] for t in range(NT)])], local_sem=T.sem.lsem)
-    lcount[0] += len(common)
-    for t in range(NT):
-        arrive("wa", len(common) * NT, "wf", 2 * t, 2 * t + 2)
+
+    def send_weights():
+        g.remote_dma_fused([RemoteDMATransfer(
+            dst_ids=[DstId(rid=topo.addr(c)[0], pnc=topo.addr(c)[1]) for c in allto], dma_engine_mask=wmask,
+            remote_sem=T.sem.wa, srcs=[T.wt[:, :]], dsts=[T.wf[:, 2 * t:2 * t + 2] for t in range(NT)])], local_sem=T.sem.lsem)
+        lcount[0] += len(common)
+
+    def arrive(sem, val, name, lo, hi, lat):
+        plan.append(("X", [lambda: arrive_now(sem, val, name, lo, hi)], [], [(name, lo, hi)], "x", lat, [sends[-1]]))
+
+    sends = [len(plan)]
+    plan.append(("G", [send_weights], [("wt", 0, 2)], [], "s", 1.0, []))
+    arrive("wa", len(common) * NT, "wf", 0, 2 * NT, 4.0)
 
     def send(dst, out_n, in_n, lo, hi, sem):
         eng = topo.engines(core, dst)[:8]
-        before("G", [(in_n, lo, hi)])
         rid, pid, _s = topo.addr(dst)
-        g.remote_dma(T[out_n][:, lo:hi], T[in_n][:, lo:hi], T.sem[sem], T.sem.lsem, pid, rid, sum(1 << e for e in eng))
-        lcount[0] += len(eng)
+
+        def call():
+            g.remote_dma(T[out_n][:, lo:hi], T[in_n][:, lo:hi], T.sem[sem], T.sem.lsem, pid, rid, sum(1 << e for e in eng))
+            lcount[0] += len(eng)
+        sends.append(len(plan))
+        plan.append(("G", [call], [(in_n, lo, hi)], [], "s", 1.0, []))
 
     ms(o("X", 2048, 4080), 0.0)
     ms(o("X", 4080, 4096), 512.0)
     ms(o("Ef", 2048, 2816), 4095.0)
     for n in ("PW1", "PW2", "P1s", "FP"):
         ms(o(n), 0.0)
-    ms(o("ones"), 1.0)
     cp(o("voff"), o("sp"))
     ts(o("vm"), o("sp"), -1408.0, A.add)
     ts(o("vp1"), o("sp"), 1.0, A.add)
@@ -258,7 +372,6 @@ def rank_program(g, core, T, topo):
     ts(o("NI4"), o("ia", 0, 128), 1024.0, A.is_equal, -1.0 / 4096, A.mult)
     ts(o("PI4"), o("ia", 0, 128), 1024.0, A.is_equal, 1.0 / 4096, A.mult)
     ts(o("Idb"), o("ia", 0, 128), 1024.0, A.is_equal)
-    ts(o("Idf"), o("ia", 0, 128), 1024.0, A.is_equal)
     ts(o("Idh"), o("ia", 0, 128), 1024.0, A.is_equal)
     ts(o("ib"), o("ic", 0, 128), 4, A.arith_shift_right)
     ts(o("B16"), o("ib"), o("pb"), A.is_equal)
@@ -273,10 +386,6 @@ def rank_program(g, core, T, topo):
     ts(o("RM"), o("ic2"), 0.0, A.is_gt)
     for e_ in range(8):
         ts((T.LT[:, e_, :], [("LT", 16 * e_, 16 * e_ + 16)]), o("ic", 0, 16), o("pm"), A.is_gt)
-    ts(o("cva"), o("dgS", 0, 1), -2048.0, A.mult)
-    ts(o("cvb"), o("dgS", 1, 2), 0.5, A.mult)
-    tt(o("cvc"), o("cva"), o("cvb"), A.add)
-    ts(o("cneg"), o("ones"), o("cvc"), A.mult)
     ts(o("c88"), o("RM"), 0.0, A.mult, 88.0625, A.add)
     for m in range(16):
         ts(o("Sm", 128 * m, 128 * m + 128), o("B16h"), o("dgS", m, m + 1), A.mult)
@@ -306,16 +415,16 @@ def rank_program(g, core, T, topo):
         cp(o("offs", lo, hi), o("Ci", lo, hi))
 
     def hash_mod(U, n, w):
-        act(o("hb", 128 * w, 128 * w + 2 * n), o(U, 0, 2 * n), F.Identity, bias=BIGM)
-        act(o("sb", 128 * w, 128 * w + 2 * n), o(U, 0, 2 * n), F.Identity, bias=2047.5)
-        act(o("t2", 128 * w, 128 * w + 2 * n), o("hb", 128 * w, 128 * w + 2 * n), F.Identity, bias=-BIGM)
-        mm(o(U, 256, 256 + 2 * n), o("Idf"), o("sb", 128 * w, 128 * w + 2 * n), True, False)
-        mm(o(U, 256, 256 + 2 * n), o("NegI"), o("t2", 128 * w, 128 * w + 2 * n), False, True)
-        act(o("u1s", 64 * w, 64 * w + n), o(U, 256, 256 + n), F.Copy)
+        c = (128 * w, 128 * w + 2 * n)
+        act(o("sb", *c), o(U, 0, 2 * n), F.Identity, bias=-2047.5)
+        act(o("hb", *c), o("sb", *c), F.Identity, bias=BIGM)
+        act(o("t2", *c), o("hb", *c), F.Identity, bias=-BIGM)
 
     def hash_end(U, n, w, out):
         c = (64 * w, 64 * w + n)
-        u2 = o(U, 256 + n, 256 + 2 * n)
+        u2 = o(U, n, 2 * n)
+        tt(u2, u2, o("t2", 128 * w + n, 128 * w + 2 * n), A.subtract)
+        tt(o("u1s", *c), o(U, 0, n), o("t2", 128 * w, 128 * w + n), A.subtract)
         tt(o("Pi", *c), o("u1s", *c), u2, A.mult)
         ts(o("Pd", *c), o("Pi", *c), 5, A.arith_shift_right, 2047, A.bitwise_and)
         tt(o("He", *c), o("Pd", *c), u2, A.add)
@@ -337,10 +446,8 @@ def rank_program(g, core, T, topo):
         def usum(c, j):
             lo, hi = CH[c]
             U = UB[c]
-            if j == 0:
-                mm(o(U, 0, 128), o("B16"), o("cneg"), True, False)
             for k in range(16):
-                mm(o(U, 64 * j, 64 * j + 64), window("PW%d" % (j + 1), k), o("D", 16 * lo + k, 16 * hi, 16), False, j == 1 and k == 15)
+                mm(o(U, 64 * j, 64 * j + 64), window("PW%d" % (j + 1), k), o("D", 16 * lo + k, 16 * hi, 16), k == 0, k == 15)
 
         def BG(c):
             lo, hi = CH[c]
@@ -378,10 +485,9 @@ def rank_program(g, core, T, topo):
         if t > 0:
             gather_slots(t, 64, 192)
         act(o("xc"), ind("X", 0, 4096, o("offs", 128, 192)), F.Copy)
-        mm(o("U1", 0, 24), o("B16"), o("cneg", 0, 24), True, False)
         for j in range(2):
             for m in range(16):
-                mm(o("U1", 12 * j, 12 * j + 12), window("FP", m, 144 * (2 * t + j)), o("z", m, 192, 16), False, j == 1 and m == 15)
+                mm(o("U1", 12 * j, 12 * j + 12), window("FP", m, 144 * (2 * t + j)), o("z", m, 192, 16), m == 0, m == 15)
         XG(0)
         for f in deferred:
             f()
@@ -394,8 +500,7 @@ def rank_program(g, core, T, topo):
         ts(o("Ki"), o("ev"), 12, A.arith_shift_right)
         hash_end("U1", 12, 3, o("zq", 12 * t, 12 * t + 12))
         send(b, "qi", "zq", 12 * t, 12 * t + 12, "qa%d" % t)
-        arrive("qa%d" % t, len(topo.engines(asker, core)[:8]), "qi", 12 * t, 12 * t + 12)
-        arrive("ra%d" % t, len(topo.engines(b, core)[:8]), "yi", L * t, L * t + L)
+        arrive("qa%d" % t, len(topo.engines(asker, core)[:8]), "qi", 12 * t, 12 * t + 12, 3.5)
         for hf in range(2):
             bank = ("TB", "S1")[hf]
             mm(o(bank), o("Idb"), o("xc", 512 * hf, 512 * hf + 512), True, False)
@@ -429,6 +534,7 @@ def rank_program(g, core, T, topo):
         over(1)
         act(o("yo", L * t, L * t + L), ind("bk3", 0, 6144, o("qi", 12 * t, 12 * t + 12)), F.Copy)
         send(asker, "yi", "yo", L * t, L * t + L, "ra%d" % t)
+        arrive("ra%d" % t, len(topo.engines(b, core)[:8]), "yi", L * t, L * t + L, 4.5)
         act(o("O", 192, 320), o("O", 0, 128), F.Relu, scale=-128.0, bias=1216.0)
         hash_end("U0", 64, 2, o("h", 128, 192))
         BG(2)
@@ -477,13 +583,13 @@ def rank_program(g, core, T, topo):
             def d4():
                 for c in range(c0, c1):
                     ts((T.EQ[:, c, 0:L - 16 * c], [("EQ", L * c, L * c + L - 16 * c)]), o("CB", 16 * c, L), o("vlw", c, c + 1), A.is_equal)
-                eqd = (T.EQ[:, c0:c1, 0:16], [("EQ", L * c0, L * c1)])
+                eqd = (T.EQ[:, c0:c1, 0:16], [("EQ", L * c0, L * c1)], 16 * (c1 - c0))
                 tt(eqd, eqd, (T.LT[:, 0:c1 - c0, :], [("LT", 0, 16 * (c1 - c0))]), A.mult)
 
                 def count(cs, x0, x1, first, final):
                     for c in cs:
                         s = max(x0, 16 * c)
-                        mm(o("CB", 192 + s, 192 + x1), o("B16"), (T.EQ[:, c, s - 16 * c:x1 - 16 * c], [("EQ", L * c, L * c + L)]),
+                        mm(o("CB", 192 + s, 192 + x1), o("B16"), (T.EQ[:, c, s - 16 * c:x1 - 16 * c], [("EQ", L * c, L * c + L)], x1 - s),
                            first and c == cs[0], final and c == cs[-1])
                 if lo == 0:
                     count(list(range(8)), 0, 128, True, True)
@@ -579,5 +685,18 @@ def rank_program(g, core, T, topo):
         else:
             deferred.extend((C[8], C[6]))
 
+    if "order" not in ORDER:
+        ORDER["order"] = schedule(plan)
+    for i in ORDER["order"]:
+        q, calls, reads, writes, kind, _d, _a = plan[i]
+        if kind == "x":
+            calls[0]()
+        elif kind == "s":
+            before("G", reads)
+            calls[0]()
+        else:
+            for c in calls[:-1]:
+                emit_now(q, c, reads, writes)
+            emit_now(q, calls[-1], reads, writes, dma=kind == "d")
     finish()
     g.wait_ge(T.sem.lsem, lcount[0])

import math
from concourse.bass import DstId, RemoteDMATransfer
from concourse.mybir import AluOpType as A, ActivationFunctionType as F

N = 8
M, L, NT = 2048, 192, 4
W = M + L * NT
BIGM = 1.5 * 2.0 ** 35
LN32 = math.log(32.0)

SCRATCH = {
    "kI": ("sbuf", [128, 2048], "int32"), "Ef": ("sbuf", [128, 2816], "float32"),
    "X": ("sbuf", [128, 4096], "bfloat16"), "bk3": ("sbuf", [128, 6144], "bfloat16"),
    "x": ("sbuf", [128, 192], "bfloat16"), "sp": ("sbuf", [128, 12], "int32"), "wt": ("sbuf", [128, 2], "bfloat16"),
    "ia": ("sbuf", [128, 192], "int32"), "ic": ("sbuf", [128, 192], "int32"), "ic2": ("sbuf", [128, 192], "int32"),
    "ib": ("sbuf", [128, 128], "int32"), "dgi": ("sbuf", [128, 192], "int32"), "i8": ("sbuf", [128, 8], "int32"),
    "p0": ("sbuf", [128, 1], "int32"), "p1": ("sbuf", [128, 1], "int32"), "p2": ("sbuf", [128, 1], "int32"),
    "pm": ("sbuf", [128, 1], "float32"), "pb": ("sbuf", [128, 1], "float32"),
    "nci": ("sbuf", [128, 768], "int32"), "NC": ("sbuf", [128, 768], "float16"),
    "dli": ("sbuf", [128, 48], "int32"), "DL": ("sbuf", [128, 48], "float32"), "DLm": ("sbuf", [128, 48], "float32"),
    "dgS": ("sbuf", [128, 192], "bfloat16"), "LT": ("sbuf", [128, 8, 16], "bfloat16"),
    "NegI": ("sbuf", [128, 128], "bfloat16"), "NI4": ("sbuf", [128, 128], "bfloat16"),
    "PI4": ("sbuf", [128, 128], "bfloat16"), "Idb": ("sbuf", [128, 128], "bfloat16"), "xc": ("sbuf", [128, 1024], "bfloat16"),
    "Idh": ("sbuf", [128, 128], "float16"), "B16": ("sbuf", [128, 128], "bfloat16"),
    "B16h": ("sbuf", [128, 128], "float16"), "B4h": ("sbuf", [128, 128], "float16"),
    "BT": ("sbuf", [128, 128], "bfloat16"), "Tri": ("sbuf", [128, 128], "bfloat16"),
    "tri0": ("sbuf", [128, 128], "bfloat16"), "G8": ("sbuf", [128, 8], "bfloat16"),
    "Sm": ("sbuf", [128, 2048], "float16"), "RM": ("sbuf", [128, 192], "float32"),
    "c88": ("sbuf", [128, 192], "float16"),
    "PW1": ("sbuf", [128, 143], "bfloat16"), "PW2": ("sbuf", [128, 143], "bfloat16"), "P1s": ("sbuf", [128, 143], "bfloat16"),
    "voff": ("sbuf", [128, 12], "uint16"), "soff": ("sbuf", [128, 12], "uint16"), "vm": ("sbuf", [128, 12], "float32"),
    "vp1": ("sbuf", [128, 12], "float32"), "vmh": ("sbuf", [128, 12], "float16"), "vmd": ("sbuf", [128, 12], "float32"),
    "bki": ("sbuf", [128, 12], "int32"), "bka": ("sbuf", [128, 12], "int32"), "bkf": ("sbuf", [128, 12], "float32"),
    "bmv": ("sbuf", [128, 12], "float32"), "vlw": ("sbuf", [128, 12], "float32"), "ta": ("sbuf", [128, 12], "float32"),
    "tb": ("sbuf", [128, 12], "float32"), "tc": ("sbuf", [128, 12], "float32"), "ts": ("sbuf", [128, 12], "float32"),
    "ts2": ("sbuf", [128, 12], "float32"), "vfin": ("sbuf", [128, 12], "float32"),
    "ev": ("sbuf", [128, 192], "int32"), "Ci": ("sbuf", [128, 192], "int32"), "offs": ("sbuf", [128, 192], "uint16"),
    "xr": ("sbuf", [128, 2048], "bfloat16"), "diff": ("sbuf", [128, 3072], "bfloat16"),
    "D": ("sbuf", [128, 3072], "bfloat16"), "sg": ("sbuf", [128, 3072], "bfloat16"), "cmp": ("sbuf", [128, 3072], "bfloat16"),
    "zd": ("sbuf", [128, 192], "bfloat16"), "z": ("sbuf", [128, 192], "bfloat16"),
    "hb": ("sbuf", [128, 512], "float32"), "sb": ("sbuf", [128, 512], "float32"), "t2": ("sbuf", [128, 512], "bfloat16"), "u1s": ("sbuf", [128, 256], "float32"),
    "Pi": ("sbuf", [128, 256], "int32"), "Pd": ("sbuf", [128, 256], "int32"), "He": ("sbuf", [128, 256], "float32"),
    "h": ("sbuf", [128, 192], "uint16"),
    "Ki": ("sbuf", [128, 192], "int32"), "emp": ("sbuf", [128, 192], "bfloat16"), "edg": ("sbuf", [128, 192], "bfloat16"),
    "K2": ("sbuf", [128, 192], "float32"), "Cf": ("sbuf", [128, 192], "float16"), "bigK": ("sbuf", [128, 192], "float32"),
    "CN": ("sbuf", [128, 384], "bfloat16"), "WW": ("sbuf", [128, 384], "bfloat16"), "isb": ("sbuf", [128, 384], "bfloat16"),
    "sel": ("sbuf", [128, 384], "bfloat16"), "pay": ("sbuf", [128, 384], "float16"),
    "wdgw": ("sbuf", [128, 192], "bfloat16"), "gdg": ("sbuf", [128, 192], "float32"), "dn": ("sbuf", [128, 192], "float32"),
    "sc1": ("sbuf", [128, 192], "float32"), "sc2": ("sbuf", [128, 192], "float32"), "sc3": ("sbuf", [128, 192], "float32"),
    "cR": ("sbuf", [128, 192], "float32"), "val": ("sbuf", [128, 192], "float32"), "wdg": ("sbuf", [128, 192], "bfloat16"),
    "q2": ("sbuf", [128, 192], "float32"), "capw": ("sbuf", [128, 192], "bfloat16"), "q3": ("sbuf", [128, 192], "float32"),
    "EQ": ("sbuf", [128, 12, 192], "bfloat16"), "xy": ("sbuf", [128, 192], "bfloat16"), "xw": ("sbuf", [128, 192], "bfloat16"),
    "dx": ("sbuf", [128, 192], "bfloat16"),
    "U0": ("psum", [128, 512], "float32"), "U1": ("psum", [128, 512], "float32"), "O": ("psum", [128, 512], "float32"),
    "S0": ("psum", [128, 512], "float32"), "S1": ("psum", [128, 512], "float32"), "TB": ("psum", [128, 512], "float32"),
    "VP": ("psum", [128, 512], "float32"), "CB": ("psum", [128, 512], "float32"),
}
SCRATCH["FP"] = ("sbuf", [128, 8 * 144], "bfloat16")
for _n, _w, _d in (("wf", 2, "bfloat16"), ("zq", 12, "uint16"), ("qi", 12, "uint16"), ("yo", 192, "bfloat16"), ("yi", 192, "bfloat16")):
    SCRATCH[_n] = ("sbuf", [128, NT * _w], _d)
PSUM = [n for n in SCRATCH if SCRATCH[n][0] == "psum"]
NDMA = 16
SEMAPHORES = ["sV", "sS", "sP", "sG", "lsem", "wa"] + ["qa%d" % t for t in range(NT)] + ["ra%d" % t for t in range(NT)] + ["d%d" % i for i in range(NDMA)]


def tracker(g, T):
    eng = {"V": g.vector, "S": g.scalar, "P": g.tensor, "G": g, "Y": g.sync}
    know = {q: {} for q in eng}
    cnt = {q: 0 for q in eng}
    wr, rd, bank, used = {}, {}, {}, [0]

    def waits(q, ops):
        k = know[q]
        ops = [o for o in ops if k.get(o[0], 0) < o[1]]
        ops.sort(key=lambda o: -len(o[2]))
        best = {}
        for o in ops:
            if o[0] not in best or best[o[0]][1] < o[1]:
                best[o[0]] = o
        ops = list(best.values())
        keep = []
        for o in ops:
            if not any(p is not o and p[2].get(o[0], 0) >= o[1] for p in ops):
                keep.append(o)
        for o in keep:
            eng[q].wait_ge(T.sem[o[0]], o[1])
        for o in keep:
            for s, v in o[2].items():
                if k.get(s, 0) < v:
                    k[s] = v

    def deps(q, reads, writes, dma):
        out = []
        for n, lo, hi in reads:
            out += [o for a, b, o in wr.get(n, []) if a < hi and lo < b]
        for n, lo, hi in writes:
            for a, b, o in wr.get(n, []):
                if a < hi and lo < b and not (o[3] == q == "P"):
                    out.append(o)
            for a, b, o in rd.get(n, []):
                if a < hi and lo < b and (o[3] != q or dma):
                    out.append(o)
        for n in set([r[0] for r in reads + writes]):
            if n in PSUM:
                out += [o for p, o in bank.get(n, {}).items() if p != q]
        if q == "P":
            out = [o for o in out if o[3] != "P"]
        return out

    def note(op, reads, writes, q):
        for n, lo, hi in writes:
            wr[n] = [e for e in wr.get(n, []) if not (lo <= e[0] and e[1] <= hi)] + [(lo, hi, op)]
            rd[n] = [e for e in rd.get(n, []) if not (lo <= e[0] and e[1] <= hi)]
        for n, lo, hi in reads:
            old = [e for e in rd.get(n, []) if not (lo <= e[0] and e[1] <= hi and e[2][3] == q and op[4] == 0 and e[2][4] == 0)]
            rd[n] = old + [(lo, hi, op)]
        for n in set([r[0] for r in reads + writes]):
            if n in PSUM:
                bank.setdefault(n, {})[q] = op

    def emit(q, call, reads, writes, dma=False):
        waits(q, deps(q, reads, writes, dma))
        ins = call(eng[q])
        if dma:
            s, v = "d%d" % used[0], 16
            used[0] += 1
        else:
            cnt[q] += 1
            s, v = "s" + q, cnt[q]
        ins.then_inc(T.sem[s], 16 if dma else 1)
        clk = dict(know[q])
        clk[s] = v
        note((s, v, clk, "d" if dma else q, 1 if dma else 0), reads, writes, q)

    def arrive(sem, val, name, lo, hi):
        note((sem, val, {sem: val}, "X", 1), [], [(name, lo, hi)], "X")

    def before(q, reads):
        waits(q, deps(q, reads, [], True))

    def finish():
        for q in eng:
            if cnt[q]:
                g.wait_ge(T.sem["s" + q], cnt[q])
        for i in range(used[0]):
            g.wait_ge(T.sem["d%d" % i], 16)
    return emit, arrive, before, finish


WAKE, SELF = 0.10, 0.10


def schedule(plan):
    n = len(plan)
    pred = [{} for _ in range(n)]
    succ = [{} for _ in range(n)]
    wr, rd = {}, {}

    def edge(a, b, lat):
        if a != b and pred[b].get(a, -1.0) < lat:
            pred[b][a] = lat
            succ[a][b] = lat
    for i, (q, _c, reads, writes, kind, _d, after) in enumerate(plan):
        for j in after:
            edge(j, i, 0.0)
        for b, lo, hi in reads:
            for x, y, j in wr.get(b, []):
                if x < hi and lo < y:
                    edge(j, i, WAKE if plan[j][0] != q or kind == "d" else 0.0 if q == "P" else SELF)
        for b, lo, hi in writes:
            for x, y, j in wr.get(b, []) + rd.get(b, []):
                if x < hi and lo < y:
                    edge(j, i, WAKE if plan[j][0] != q else 0.0)
        for b, lo, hi in writes:
            wr[b] = [e for e in wr.get(b, []) if not (lo <= e[0] and e[1] <= hi)] + [(lo, hi, i)]
            rd[b] = [e for e in rd.get(b, []) if not (lo <= e[0] and e[1] <= hi)]
        for b, lo, hi in reads:
            rd.setdefault(b, []).append((lo, hi, i))
    left = [len(p) for p in pred]
    end = [0.0] * n
    early = [0.0] * n
    free, bank, dfree = {}, {}, 0.0
    banks = [sorted(set(b for b, _l, _h in p[2] + p[3] if b in PSUM)) for p in plan]
    ready = [i for i in range(n) if left[i] == 0]
    order = []
    while ready:
        best = None
        for i in ready:
            q = plan[i][0]
            t = max(early[i], free.get(q, 0.0)) if q != "X" else early[i]
            for b in banks[i]:
                for q2, e in bank.get(b, {}).items():
                    if q2 != q and e + WAKE > t:
                        t = e + WAKE
            key = (round(t / SLOT), i)
            if best is None or key < best[0]:
                best = (key, i, t)
        _k, i, t = best
        ready.remove(i)
        order.append(i)
        q, kind, d = plan[i][0], plan[i][4], plan[i][5]
        if kind == "d":
            free[q] = t + 0.1
            dfree = max(dfree, t + 1.0) + d
            end[i] = dfree + 1.0
        else:
            end[i] = t + d
            free[q] = end[i]
        for b in banks[i]:
            bank.setdefault(b, {})[q] = end[i]
        for j, lat in succ[i].items():
            early[j] = max(early[j], end[i] + lat)
            left[j] -= 1
            if left[j] == 0:
                ready.append(j)
    return order


SLOT = 0.02
ORDER = {}


def rank_program(g, core, T, topo):
    r = T.rank_of(core)
    if r is None:
        return
    emit_now, arrive_now, before, finish = tracker(g, T)
    plan = []

    def emit(q, call, reads, writes, dma=False, dur=0.06):
        plan.append((q, [call], reads, writes, "d" if dma else "c", dur, []))

    def cols(x):
        return x[2] if len(x) > 2 else x[1][0][2] - x[1][0][1]

    def dt_of(x):
        return SCRATCH.get(x[1][0][0], ("sbuf", 0, "bfloat16"))[2]

    def in_psum(x):
        return x[1][0][0] in PSUM

    CYC = 0.00085

    def time_of(out, a, b=None):
        if len(a) > 3:
            return 0.06 + 1.56 * CYC * cols(out)
        if len(out) > 3:
            return 0.06 + 3.8 * CYC * cols(a)
        n = cols(out)
        if b is not None:
            f = 1.0 if in_psum(a) or in_psum(b) else 2.0
        else:
            f = 0.5 if not in_psum(a) and not in_psum(out) and dt_of(a) in TWO and dt_of(out) in TWO else 1.0
        return CYC * max(64, f * n)
    TWO = ("bfloat16", "float16", "uint16")
    group = []
    width = {n: (SCRATCH[n][1][1] if len(SCRATCH[n][1]) == 2 else SCRATCH[n][1][1] * SCRATCH[n][1][2]) for n in SCRATCH}

    def o(n, lo=0, hi=None, step=1):
        hi = width[n] if hi is None else hi
        return (T[n][:, lo:hi] if step == 1 else T[n][:, lo:hi:step], [(n, lo, hi)], (hi - lo + step - 1) // step)

    def ind(n, lo, hi, off):
        return (T[n][:, lo:hi].indirect(off[0]), [(n, lo, hi)] + off[1], 16 * off[2], "indirect")

    def sca(s):
        return (s[0], s[1]) if isinstance(s, tuple) else (s, [])

    def tt(out, a, b, op):
        emit("V", lambda e: e.tensor_tensor(out[0], a[0], b[0], op), a[1] + b[1], out[1], dur=time_of(out, a, b))

    def ts(out, a, s1, op0, s2=None, op1=None):
        s1 = sca(s1)
        if op1 is None:
            emit("V", lambda e: e.tensor_scalar(out[0], a[0], s1[0], None, op0), a[1] + s1[1], out[1], dur=time_of(out, a))
        else:
            emit("V", lambda e: e.tensor_scalar(out[0], a[0], s1[0], s2, op0, op1), a[1] + s1[1], out[1], dur=time_of(out, a))

    def cp(out, a):
        emit("V", lambda e: e.tensor_copy(out[0], a[0]), a[1] + out[1][1:], out[1][:1], dur=time_of(out, a))

    def ms(out, c):
        emit("V", lambda e: e.memset(out[0], c), [], out[1], dur=CYC * cols(out))

    def scan(out, a, b):
        emit("V", lambda e: e.tensor_tensor_scan(out[0], a[0], b[0], 0.0, A.mult, A.add), a[1] + b[1], out[1], dur=CYC * cols(out))

    def act(out, a, func, scale=1.0, bias=0.0):
        emit("S", lambda e: e.activation(out[0], a[0], func, bias=bias, scale=scale), a[1], out[1],
             dur=0.065 + CYC * cols(a) * (1.56 if len(a) > 3 else 1.0))

    def mm(out, lhsT, rhs, start, stop, whole=None, cut=False):
        group.append((lambda e: e.matmul(out[0], lhsT[0], rhs[0], start, stop), lhsT[1] + rhs[1], out[1] + ([(whole, 0, 512)] if whole else []),
                      0.0007 * max(64, cols(rhs)) * (4 if dt_of(rhs) == "float32" else 1)))
        if stop or cut:
            plan.append(("P", [c[0] for c in group], sorted(set(x for c in group for x in c[1])), sorted(set(x for c in group for x in c[2])),
                         "c", sum(c[3] for c in group), []))
            del group[:]

    def iota(n, pattern, base, cm):
        b = o(n)
        emit("G", lambda e: e.iota(b[0], pattern, base, cm), [], b[1], dur=0.15 + 2 * CYC * cols(b))

    def load(q, name, lo, hi, src):
        b = o(name, lo, hi)
        emit(q, lambda e: e.dma_start(b[0], src), [], b[1], dma=True, dur=0.0013 * cols(b) * (1 if dt_of(b) in TWO else 2))

    def store(q, dst, b):
        emit(q, lambda e: e.dma_start(dst, b[0]), b[1], [], dma=True, dur=0.0013 * cols(b) * (1 if dt_of(b) in TWO else 2))

    load("S", "wt", 0, 2, T.wts[:, :])
    load("Y", "sp", 0, 12, T.spot[:, :])
    load("Y", "kI", 0, 2048, T.kids[:, :])
    load("S", "x", 0, 192, T.cand[:, :])
    load("Y", "X", 0, 2048, T.nodes[:, :])
    for j in range(3):
        load("Y", "bk3", 2048 * j, 2048 * j + 2048, T.book[:, :])

    iota("p0", [[0, 1]], 0, 1)
    iota("ia", [[1, 192]], 1024, -1)
    iota("ic", [[1, 192]], 0, 0)
    iota("i8", [[1, 8]], 0, 0)
    iota("dli", [[16, 48]], 2048, 0)
    iota("nci", [[1, 768]], -2047, 0)

    allto = [T.cores[(r - 1 - t) % N] for t in range(NT)]
    common = [e for e in topo.engines(core, allto[0]) if all(e in topo.engines(core, c) for c in allto)][:8]
    wmask = sum(1 << e for e in common)
    lcount = [0]

    def send_weights():
        g.remote_dma_fused([RemoteDMATransfer(
            dst_ids=[DstId(rid=topo.addr(c)[0], pnc=topo.addr(c)[1]) for c in allto], dma_engine_mask=wmask,
            remote_sem=T.sem.wa, srcs=[T.wt[:, :]], dsts=[T.wf[:, 2 * t:2 * t + 2] for t in range(NT)])], local_sem=T.sem.lsem)
        lcount[0] += len(common)

    def arrive(sem, val, name, lo, hi, lat):
        plan.append(("X", [lambda: arrive_now(sem, val, name, lo, hi)], [], [(name, lo, hi)], "x", lat, [sends[-1]]))

    sends = [len(plan)]
    plan.append(("G", [send_weights], [("wt", 0, 2)], [], "s", 1.0, []))
    arrive("wa", len(common) * NT, "wf", 0, 2 * NT, 4.0)

    def send(dst, out_n, in_n, lo, hi, sem):
        eng = topo.engines(core, dst)[:8]
        rid, pid, _s = topo.addr(dst)

        def call():
            g.remote_dma(T[out_n][:, lo:hi], T[in_n][:, lo:hi], T.sem[sem], T.sem.lsem, pid, rid, sum(1 << e for e in eng))
            lcount[0] += len(eng)
        sends.append(len(plan))
        plan.append(("G", [call], [(in_n, lo, hi)], [], "s", 1.0, []))

    ms(o("X", 2048, 4080), 0.0)
    ms(o("X", 4080, 4096), 512.0)
    ms(o("Ef", 2048, 2816), 4095.0)
    for n in ("PW1", "PW2", "P1s", "FP"):
        ms(o(n), 0.0)
    cp(o("voff"), o("sp"))
    ts(o("vm"), o("sp"), -1408.0, A.add)
    ts(o("vp1"), o("sp"), 1.0, A.add)
    cp(o("vmh"), o("vm"))
    ts(o("p1"), o("p0"), 15, A.bitwise_and)
    cp(o("pm"), o("p1"))
    ts(o("p2"), o("p0"), 4, A.arith_shift_right)
    cp(o("pb"), o("p2"))
    ts(o("dgi"), o("ia"), 15, A.bitwise_and)
    ts(o("dgS"), o("dgi"), 0.0, A.is_equal)
    dgP = lambda lo, hi: o("VP", lo, hi)
    ts(o("VP", 0, 192), o("dgi"), 0.0, A.is_equal)
    ts(o("NegI"), o("ia", 0, 128), 1024.0, A.is_equal, -1.0, A.mult)
    ts(o("NI4"), o("ia", 0, 128), 1024.0, A.is_equal, -1.0 / 4096, A.mult)
    ts(o("PI4"), o("ia", 0, 128), 1024.0, A.is_equal, 1.0 / 4096, A.mult)
    ts(o("Idb"), o("ia", 0, 128), 1024.0, A.is_equal)
    ts(o("Idh"), o("ia", 0, 128), 1024.0, A.is_equal)
    ts(o("ib"), o("ic", 0, 128), 4, A.arith_shift_right)
    ts(o("B16"), o("ib"), o("pb"), A.is_equal)
    cp(o("B16h"), o("B16"))
    ts(o("B4h"), o("B16"), 4096.0, A.mult)
    ts(o("BT"), o("B16"), 3.0 / 64, A.mult)
    ts(o("tri0"), o("ia", 0, 128), 1024.0, A.is_gt)
    tt(o("Tri"), o("tri0"), o("B16"), A.mult)
    ts(o("G8"), o("i8"), o("pb"), A.is_equal)
    ts(o("P1s", 15, 143, 16), o("G8"), 1.0, A.mult)
    ts(o("ic2"), o("ic"), 15, A.bitwise_and)
    ts(o("RM"), o("ic2"), 0.0, A.is_gt)
    for e_ in range(8):
        ts((T.LT[:, e_, :], [("LT", 16 * e_, 16 * e_ + 16)]), o("ic", 0, 16), o("pm"), A.is_gt)
    ts(o("c88"), o("RM"), 0.0, A.mult, 88.0625, A.add)
    for m in range(16):
        ts(o("Sm", 128 * m, 128 * m + 128), o("B16h"), o("dgS", m, m + 1), A.mult)
    ts(o("DL"), o("dli"), o("pm"), A.add)
    ts(o("DLm"), o("DL"), -1408.0, A.add)
    cp(o("NC"), o("nci"))
    ts(o("PW1", 15, 143, 16), o("G8"), o("wt", 0, 1), A.mult)
    ts(o("PW2", 15, 143, 16), o("G8"), o("wt", 1, 2), A.mult)

    def window(n, k, base=0):
        return o(n, base + 15 - k, base + 143 - k)

    def repeat():
        for k in range(16):
            act((T.xr[:, k:2048:16], [("xr%d" % k, 0, 2048)]), o("x", 0, 128), F.Copy)

    repeat()

    CH = ((0, 64), (64, 128), (128, 192))
    UB = ("U0", "U1", "U0")
    deferred = []

    def gather_slots(t, lo, hi):
        tab = ("kI", 0, 2048) if t == 0 else ("Ef", 0, W)
        cp(o("ev", lo, hi), ind(tab[0], tab[1], tab[2], o("voff", lo // 16, hi // 16)))
        ts(o("Ci", lo, hi), o("ev", lo, hi), 4095, A.bitwise_and)
        cp(o("offs", lo, hi), o("Ci", lo, hi))

    def hash_mod(U, n, w):
        c = (128 * w, 128 * w + 2 * n)
        act(o("sb", *c), o(U, 0, 2 * n), F.Identity, bias=-2047.5)
        act(o("hb", *c), o("sb", *c), F.Identity, bias=BIGM)
        act(o("t2", *c), o("hb", *c), F.Identity, bias=-BIGM)

    def hash_end(U, n, w, out):
        c = (64 * w, 64 * w + n)
        u2 = o(U, n, 2 * n)
        tt(u2, u2, o("t2", 128 * w + n, 128 * w + 2 * n), A.subtract)
        tt(o("u1s", *c), o(U, 0, n), o("t2", 128 * w, 128 * w + n), A.subtract)
        tt(o("Pi", *c), o("u1s", *c), u2, A.mult)
        ts(o("Pd", *c), o("Pi", *c), 5, A.arith_shift_right, 2047, A.bitwise_and)
        tt(o("He", *c), o("Pd", *c), u2, A.add)
        cp(out, o("He", *c))

    for t in range(NT):
        last = t == NT - 1
        b = T.cores[(r + 1 + t) % N]
        asker = T.cores[(r - 1 - t) % N]

        def XG(c):
            lo, hi = CH[c]
            dv = o("diff", 16 * lo, 16 * hi)
            xg = ind("X", 0, 4096, o("offs", lo, hi))
            xv = (T.xr[:, 16 * lo:16 * hi], [("xr%d" % k, 16 * lo, 16 * hi) for k in range(16)])
            tt(dv, xg, xv, A.subtract)
            act(o("D", 16 * lo, 16 * hi), dv, F.Abs)

        def usum(c, j):
            lo, hi = CH[c]
            U = UB[c]
            for k in range(16):
                mm(o(U, 64 * j, 64 * j + 64), window("PW%d" % (j + 1), k), o("D", 16 * lo + k, 16 * hi, 16), k == 0, k == 15)

        def BG(c):
            lo, hi = CH[c]
            tt(o("cmp", 16 * lo, 16 * hi), ind("bk3", 0, 6144, o("h", lo, hi)), o("D", 16 * lo, 16 * hi), A.is_ge)

        def sign(c):
            lo, hi = CH[c]
            if c == 2:
                for hf in range(2):
                    act(o("sg", 2048 + 512 * hf, 2560 + 512 * hf), o(("TB", "S1")[hf]), F.Sign, scale=-1.0, bias=0.5)
            else:
                ts(o("sg", 16 * lo, 16 * hi), o("diff", 16 * lo, 16 * hi), 0.0, A.is_le)

        def over(c):
            lo, hi = CH[c]
            for k in range(16):
                mm(o("O", lo, hi), window("P1s", k), o("sg", 16 * lo + k, 16 * hi, 16), k == 0, k == 15)

        def ssum(c):
            lo, hi = CH[c]
            so = o("S0", lo, hi) if c < 2 else o("S1", 0, 64)
            mm(so, o("PI4"), o("emp", lo, hi), True, False)
            mm(so, o("NI4"), o("edg", lo, hi), False, False)
            for k in range(16):
                mm(so, window("P1s", k), o("cmp", 16 * lo + k, 16 * hi, 16), False, k == 15)

        gather_slots(t, 0, 64)
        if t == 0:
            gather_slots(t, 64, 192)
            cp(o("Ef", 0, 2048), o("kI"))
            for j in range(2 * NT):
                ts(o("FP", 144 * j + 15, 144 * j + 143, 16), o("G8"), o("wf", j, j + 1), A.mult)
        tt(o("zd"), ind("X", 0, 4096, o("voff")), o("x"), A.subtract)
        act(o("z"), o("zd"), F.Abs)
        if t > 0:
            gather_slots(t, 64, 192)
        act(o("xc"), ind("X", 0, 4096, o("offs", 128, 192)), F.Copy)
        for j in range(2):
            for m in range(16):
                mm(o("U1", 12 * j, 12 * j + 12), window("FP", m, 144 * (2 * t + j)), o("z", m, 192, 16), m == 0, m == 15)
        XG(0)
        for f in deferred:
            f()
        del deferred[:]
        usum(0, 0)
        hash_mod("U1", 12, 3)
        usum(0, 1)
        XG(1)
        ts(o("emp"), o("Ci"), 4095.0, A.is_equal, -4096.0, A.mult)
        ts(o("Ki"), o("ev"), 12, A.arith_shift_right)
        hash_end("U1", 12, 3, o("zq", 12 * t, 12 * t + 12))
        send(b, "qi", "zq", 12 * t, 12 * t + 12, "qa%d" % t)
        arrive("qa%d" % t, len(topo.engines(asker, core)[:8]), "qi", 12 * t, 12 * t + 12, 3.5)
        for hf in range(2):
            bank = ("TB", "S1")[hf]
            mm(o(bank), o("Idb"), o("xc", 512 * hf, 512 * hf + 512), True, False)
            for k in range(16):
                mm(o(bank, k, 512, 16), o("NegI"), o("x", 128 + 32 * hf, 160 + 32 * hf), False, k == 15)
        hash_mod("U0", 64, 0)
        for hf in range(2):
            act(o("D", 2048 + 512 * hf, 2560 + 512 * hf), o(("TB", "S1")[hf]), F.Abs)
        usum(1, 0)
        usum(1, 1)
        sign(0)
        tt(o("edg"), dgP(0, 192), o("emp"), A.mult)
        ts(o("Cf"), o("Ci"), -1408.0, A.add)
        tt(o("K2"), o("Ki"), o("edg"), A.add)
        hash_end("U0", 64, 0, o("h", 0, 64))
        BG(0)
        hash_mod("U1", 64, 1)
        usum(2, 0)
        usum(2, 1)
        sign(2)
        ts(o("VP", 256, 448), o("ev"), -1.0, A.mult, 4095.0, A.add)
        hash_end("U1", 64, 1, o("h", 64, 128))
        BG(1)
        mm(o("CB", 0, 192), o("B16h"), o("c88"), True, False)
        for m in range(16):
            mm(o("CB", m, 192, 16), o("Sm", 128 * m, 128 * m + 128), o("vmh"), False, m == 15)
        over(0)
        hash_mod("U0", 64, 2)
        ssum(0)
        sign(1)
        over(1)
        act(o("yo", L * t, L * t + L), ind("bk3", 0, 6144, o("qi", 12 * t, 12 * t + 12)), F.Copy)
        send(asker, "yi", "yo", L * t, L * t + L, "ra%d" % t)
        arrive("ra%d" % t, len(topo.engines(b, core)[:8]), "yi", L * t, L * t + L, 4.5)
        act(o("O", 192, 320), o("O", 0, 128), F.Relu, scale=-128.0, bias=1216.0)
        hash_end("U0", 64, 2, o("h", 128, 192))
        BG(2)
        ssum(1)
        tt(o("vmd"), o("vm"), o("DLm", 12 * t, 12 * t + 12), A.subtract)

        def batch(lo, hi, SB, t=t, last=last):
            n = hi - lo
            c0, c1 = lo // 16, hi // 16
            a, e = 2 * lo, 2 * lo + n
            z_ = 2 * hi
            T0, L0, W0 = (0, 256, 256) if lo == 0 else (384, 384, 0)
            S = o(SB, 0, n)
            EX = o(SB, n, 2 * n)
            Q1 = o(SB, 2 * n, 3 * n)
            last_lane = lambda nm: o(nm, lo + 15, hi, 16)
            lst = lambda nm: o(nm, c0, c1)

            def d1():
                act(EX, S, F.Exp, scale=LN32)
                act(Q1, S, F.Identity, scale=4096.0, bias=-4095.0)
                tt(o("bigK", lo, hi), o("O", 192 + lo, 192 + hi), o("K2", lo, hi), A.add)
                tt(o("CN", e, z_), S, o("bigK", lo, hi), A.is_gt)
                tt(o("CN", a, e), S, o("bigK", lo, hi), A.is_le)
                tt(o("WW", a, e), EX, o("CN", a, e), A.mult)
                tt(o("WW", e, z_), EX, o("CN", e, z_), A.mult)
                mm(o("TB", T0, T0 + 2 * n), o("BT"), o("WW", a, z_), True, True)

            def d2():
                tt(o("wdgw", lo, hi), dgP(lo, hi), o("CN", e, z_), A.mult)
                scan(o("sc1", lo, hi), o("RM", lo, hi), o("wdgw", lo, hi))
                tt(o("isb", a, z_), o("WW", a, z_), o("TB", T0, T0 + 2 * n), A.is_gt)
                mm(o("TB", L0, L0 + 2 * n), o("Tri"), o("isb", a, z_), True, True)

            def d3():
                tt(lst("vlw"), last_lane("sc1"), lst("vp1"), A.mult)
                tt(o("gdg", lo, hi), dgP(lo, hi), o("CN", a, e), A.mult)
                tt(Q1, Q1, o("Ci", lo, hi), A.add)
                tt(o("sel", a, z_), o("isb", a, z_), o("TB", L0, L0 + 2 * n), A.is_gt)
                tt(o("pay", e, z_), S, o("sel", e, z_), A.mult)
                tt(o("pay", a, e), o("sel", a, e), o("Cf", lo, hi), A.mult)
                mm(o("TB", T0 + n, T0 + 2 * n), o("Idh"), o("NC", L * t + lo, L * t + hi), True, False)
                mm(o("TB", T0 + n, T0 + 2 * n), o("B4h"), o("pay", e, z_), False, True)
                mm(o("TB", T0, T0 + n), o("B16h"), o("pay", a, e), True, True)

            def d4():
                for c in range(c0, c1):
                    ts((T.EQ[:, c, 0:L - 16 * c], [("EQ", L * c, L * c + L - 16 * c)]), o("CB", 16 * c, L), o("vlw", c, c + 1), A.is_equal)
                eqd = (T.EQ[:, c0:c1, 0:16], [("EQ", L * c0, L * c1)], 16 * (c1 - c0))
                tt(eqd, eqd, (T.LT[:, 0:c1 - c0, :], [("LT", 0, 16 * (c1 - c0))]), A.mult)

                def count(cs, x0, x1, first, final):
                    for c in cs:
                        s = max(x0, 16 * c)
                        mm(o("CB", 192 + s, 192 + x1), o("B16"), (T.EQ[:, c, s - 16 * c:x1 - 16 * c], [("EQ", L * c, L * c + L)], x1 - s),
                           first and c == cs[0], final and c == cs[-1])
                if lo == 0:
                    count(list(range(8)), 0, 128, True, True)
                else:
                    count(list(range(12)), 128, 192, True, True)

            def d5():
                tt(o("VP", 256 + lo, 256 + hi), o("VP", 256 + lo, 256 + hi), o("CN", e, z_), A.mult)
                tt(o("VP", 256 + lo, 256 + hi), o("VP", 256 + lo, 256 + hi), o("ev", lo, hi), A.add)
                tt(o("wdg", lo, hi), o("wdgw", lo, hi), o("CB", 192 + lo, 192 + hi), A.is_gt)
                mm(o("TB", W0, W0 + n), o("B16"), o("wdg", lo, hi), True, True)
                scan(o("sc3", lo, hi), o("RM", lo, hi), o("wdg", lo, hi))
                tt(lst("ts"), last_lane("sc3"), lst("vmd"), A.mult)
                tt(o("dn", lo, hi), o("TB", T0, T0 + n), o("gdg", lo, hi), A.mult)
                tt(lst("ts2"), lst("ts"), o("DL", 12 * t + c0, 12 * t + c1), A.add)
                tt(o("cR", lo, hi), o("TB", T0 + n, T0 + 2 * n), o("dgS", lo, hi), A.mult)
                cp(lst("soff"), lst("ts2"))
                scan(o("sc2", lo, hi), o("RM", lo, hi), o("dn", lo, hi))
                tt(o("val", lo, hi), o("VP", 256 + lo, 256 + hi), o("cR", lo, hi), A.add)
                tt(lst("ta"), last_lane("sc1"), lst("vm"), A.mult)
                cp(ind("Ef", 0, W, lst("soff")), o("val", lo, hi))
                tt(lst("tb"), lst("ta"), last_lane("sc2"), A.add)

            def d8():
                tt(lst("tc"), last_lane("sc3"), lst("bmv"), A.mult)
                tt(lst("vm"), lst("tb"), lst("tc"), A.add)
                if last:
                    ts(lst("vfin"), lst("vm"), 1408.0, A.add)
                else:
                    ts(lst("voff"), lst("vm"), 1408.0, A.add)

            def d6():
                WR = o("TB", W0, W0 + n)
                nl = M + L * t
                tt(o("VP", 256 + lo, 256 + hi), WR, o("dx", lo, hi), A.mult)
                tt(o("X", nl + lo, nl + hi), WR, o("x", lo, hi), A.mult)
                tt(o("x", lo, hi), o("VP", 256 + lo, 256 + hi), o("x", lo, hi), A.add)
                if not last and lo == 0:
                    repeat()

            def d7():
                nl = M + L * t
                tt(o("capw", lo, hi), o("TB", W0, W0 + n), o("CN", e, z_), A.mult)
                tt(o("q3", lo, hi), Q1, o("capw", lo, hi), A.mult)
                act(o("Ef", nl + lo, nl + hi), o("q3", lo, hi), F.Identity, bias=4095.0)

            def d9():
                cp(lst("vmh"), lst("vm"))
                ts(lst("vp1"), lst("vm"), 1409.0, A.add)
            return d1, d2, d3, d4, d5, d6, d7, d8, d9

        AB = batch(0, 128, "S0")
        C = batch(128, 192, "S1")
        ssum(2)
        AB[0]()
        over(2)
        act(o("O", 320, 384), o("O", 128, 192), F.Relu, scale=-64.0, bias=192.0)
        AB[1]()
        AB[2]()
        C[0]()
        mm(o("O", 0, 192), o("Idb"), o("x"), True, False)
        mm(o("O", 0, 192), o("NegI"), o("yi", L * t, L * t + L), False, True)
        act(o("xw"), o("O", 0, 192), F.Abs)
        AB[3]()
        C[1]()
        mm(o("O", 0, 192), o("Idb"), o("xw"), True, False)
        mm(o("O", 0, 192), o("NegI"), o("x"), False, True)
        act(o("dx"), o("O", 0, 192), F.Copy)
        for m in range(16):
            mm(o("O", 384, 396), window("PW1", m), o("xw", m, 192, 16), m == 0, m == 15)
        C[2]()
        AB[4]()
        cp(o("bki"), o("O", 384, 396))
        ts(o("bka"), o("bki"), 1023, A.bitwise_and)
        C[3]()
        ts(o("bkf"), o("bka"), 1.0, A.add)
        AB[6]()
        tt(o("bmv"), o("bkf"), o("vp1"), A.subtract)
        AB[5]()
        AB[7]()
        C[4]()
        C[7]()
        C[5]()
        if not last:
            AB[8]()
        if last:
            store("Y", T.ykids[:, 0:W - L], o("Ef", 0, W - L))
            C[6]()
            store("S", T.ykids[:, W - L:W], o("Ef", W - L, W))
            store("Y", T.ynodes[:, :], o("X", M, W))
            store("S", T.ycand[:, :], o("x"))
            store("Y", T.yspot[:, :], o("vfin"))
        else:
            deferred.extend((C[8], C[6]))

    if "order" not in ORDER:
        ORDER["order"] = schedule(plan)
    for i in ORDER["order"]:
        q, calls, reads, writes, kind, _d, _a = plan[i]
        if kind == "x":
            calls[0]()
        elif kind == "s":
            before("G", reads)
            calls[0]()
        else:
            for c in calls[:-1]:
                emit_now(q, c, reads, writes)
            emit_now(q, calls[-1], reads, writes, dma=kind == "d")
    finish()
    g.wait_ge(T.sem.lsem, lcount[0])
